import numpy as np
import ml_dtypes


def mxq(x, axis, fmt="e4m3"):
    dtype, down = {"e4m3": (ml_dtypes.float8_e4m3fn, 7), "e5m2": (ml_dtypes.float8_e5m2, 14)}[fmt]
    v = np.moveaxis(np.asarray(x, np.float32).astype(ml_dtypes.bfloat16).astype(np.float64), axis, -1)
    blocks = v.reshape(v.shape[:-1] + (-1, 32))
    amax = np.abs(blocks).max(-1, keepdims=True)
    byte = np.maximum(np.where(amax > 0, np.frexp(amax)[1] - 1 + 127, 0) - down, 1)
    scale = np.exp2(byte - 127.0)
    codes = (blocks / scale).astype(np.float32).astype(dtype).astype(np.float64)
    return np.moveaxis((codes * scale).reshape(v.shape), -1, axis)


WIDE = False


def mx_kscale(k):
    if not WIDE:
        return np.ones(k)
    levels = np.array([10, -10, 5, -5, 0])
    if k % 512:
        return np.exp2(np.random.permutation(np.resize(levels, k // 32))).repeat(32)
    a = np.empty((k // 512, 16))
    for p in range(k // 512):
        a[p, :8] = np.random.permutation(np.resize(levels, 8))
        for g in range(8):
            far = levels[np.abs(levels - a[p, g]) >= 10]
            a[p, g + 8] = far[np.random.randint(len(far))]
    return np.exp2(a.ravel()).repeat(32)


def f64(x):
    return np.asarray(x).astype(np.float64)


def striped(idx):
    return np.tile(np.asarray(idx).reshape(-1, 16).T, (8, 1)).astype(np.uint16)


def unstriped(offs):
    return offs[:16].T.reshape(-1).astype(np.int64)


B, N, T, D, DV, NQ = 1, 512, 2048, 512, 256, 256


def setup_inputs():
    n = np.random.standard_normal
    idx = np.sort(np.random.permutation(T)[:B * N].reshape(B, N), axis=1).reshape(-1)
    s = mx_kscale(D)[:, None]
    u = np.ones(T)
    u[idx] = mx_kscale(B * N)
    r = np.random.uniform(0.5, 2.0, T)
    k = n((D, T)) / s
    v = n((DV, T)) / (u * r)
    when = np.zeros(T)
    when[idx] = np.sort(np.random.permutation(2 * N)[:B * N])
    return {
        "qT": (n((B, D, NQ)) * s * (1.00 / np.sqrt(D))).astype(np.float32),
        "kT": k.astype(np.float32),
        "vT": v.astype(np.float32),
        "vs": np.tile(u * r, (128, 1)).astype(np.float32),
        "pos": np.tile(when, (128, 1)).astype(np.float32),
        "slope": np.exp2(-np.random.randint(8, 13, (B, NQ, 1))).astype(np.float32),
        "sink": (2.0 + 3.0 * n((B, NQ, 1))).astype(np.float32),
        "offs": striped(idx),
    }


def reference(qT, kT, vT, vs, pos, slope, sink, offs):
    idx = unstriped(offs)
    k = f64(kT)
    v = f64(vT)
    pick = lambda x: x[:, idx].reshape(x.shape[0], B, N).transpose(1, 0, 2)
    q = f64(qT)
    score = mxq(q, 1, "e4m3").transpose(0, 2, 1) @ mxq(pick(k), 1, "e4m3")
    score = score + f64(slope) * pick(f64(pos))[:, :1, :]
    m = np.maximum(score.max(-1, keepdims=True), f64(sink))
    p = np.exp(score - m)
    total = p.sum(-1, keepdims=True) + np.exp(f64(sink) - m)
    w = p * pick(f64(vs))[:, :1, :]
    y = mxq(w, 2, "e4m3") @ mxq(pick(v).transpose(0, 2, 1), 1, "e4m3")
    y = y / total
    return y

@@ -1,0 +1,234 @@
+from contextlib import ExitStack
+
+import concourse.mybir as mybir
+from concourse.masks import make_identity
+
+F32 = mybir.dt.float32
+BF16 = mybir.dt.bfloat16
+U32 = mybir.dt.uint32
+U16 = mybir.dt.uint16
+U8 = mybir.dt.uint8
+FP8X4 = mybir.dt.float8_e4m3fn_x4
+ACT = mybir.ActivationFunctionType
+ALU = mybir.AluOpType
+
+P = 128
+D, NQ, N, T, DV = 512, 256, 512, 2048, 256
+QB = NQ // P
+VB = DV // P
+FLOPS = 2 * NQ * N * (D + DV)
+BYTES = 4 * (D * NQ + D * T + DV * T + 2 * T + 2 * NQ + NQ * DV) + 2 * P * (N // 16)
+
+
+def tile_attend_x_alibi_sink_srt_kernel(tc, qT, kT, vT, vs, pos, slope, sink, offs, out):
+    nc = tc.nc
+    with ExitStack() as ctx:
+        keep = ctx.enter_context(tc.tile_pool(name="keep", bufs=1))
+        psum = ctx.enter_context(tc.psum_pool(name="psum", bufs=1))
+
+        offsets = keep.tile([P, N // 16], U16, name="offsets")
+        k_raw = [keep.tile([P, T], F32, name=f"k_raw{t}") for t in range(4)]
+        q_raw = keep.tile([P, 4, NQ], F32, name="q_raw")
+        v_raw = [keep.tile([P, T], F32, name=f"v_raw{b}") for b in range(VB)]
+        rows = keep.tile([P, P], F32, name="rows")
+        pos_raw = keep.tile([P, T], F32, name="pos_raw")
+        vs_raw = keep.tile([P, T], F32, name="vs_raw")
+        k_planes = kT.rearrange("(p t) n -> p t n", t=4)
+        nc.sync.dma_start(k_raw[0][:], k_planes[:, 0, :])
+        nc.sync.dma_start(offsets[:], offs)
+        nc.sync.dma_start(k_raw[1][:], k_planes[:, 1, :])
+
+        warm = keep.tile([P, 1], F32, name="warm")
+        nc.vector.memset(warm[:], 0.0)
+        nc.scalar.activation(warm[:], warm[:], ACT.Exp)
+
+        nc.vector.memset(rows[:], 0.0)
+        nc.sync.dma_start(rows[0:2, :], slope.rearrange("o (b p) x -> (o b) (p x)", p=P))
+        nc.sync.dma_start(rows[2:4, :], sink.rearrange("o (b p) x -> (o b) (p x)", p=P))
+        nc.vector.memset(pos_raw[:], 0.0)
+        nc.sync.dma_start(pos_raw[0:1, :], pos[0:1, :])
+        nc.vector.memset(vs_raw[:], 0.0)
+        nc.sync.dma_start(vs_raw[0:1, :], vs[0:1, :])
+        for t in (2, 3):
+            nc.sync.dma_start(k_raw[t][:], k_planes[:, t, :])
+        nc.sync.dma_start(q_raw[:], qT.rearrange("o (p t) n -> p (o t) n", t=4))
+        for b in range(VB):
+            nc.sync.dma_start(v_raw[b][:], vT[b * P : (b + 1) * P, :])
+
+        ident = keep.tile([P, P], F32, name="ident")
+        make_identity(nc, ident[:])
+        ident_bf = keep.tile([P, P], BF16, name="ident_bf")
+        nc.gpsimd.tensor_copy(ident_bf[:], ident[:])
+
+        k_bf = keep.tile([P, N, 4], BF16, align_bytes=64, name="k_bf")
+        for t in (0, 1):
+            nc.vector.tensor_copy(k_bf[:, :, t], k_raw[t][:].indirect(offsets[:]))
+
+        s = [keep.tile([P, N + 4], F32, name=f"s{b}") for b in range(QB)]
+        cols_ps = psum.tile([P, P], F32, tag="s00", name="cols_ps")
+        nc.tensor.transpose(cols_ps[:], rows[:], ident[:])
+        slope_col = keep.tile([P, QB], F32, name="slope_col")
+        nc.scalar.copy(slope_col[:], cols_ps[:, 0:QB])
+        for b in range(QB):
+            nc.scalar.copy(s[b][:, N : N + 1], cols_ps[:, QB + b : QB + b + 1])
+
+        pos_g = keep.tile([P, N], F32, name="pos_g")
+        nc.vector.tensor_copy(pos_g[:], pos_raw[:].indirect(offsets[:]))
+        posT_ps = psum.tile([P, 4, P], F32, tag="p0", name="posT_ps")
+        for t in range(4):
+            nc.tensor.transpose(posT_ps[:, t, :], pos_g[:, t::4], ident[:])
+        posT = keep.tile([P, 4], F32, name="posT")
+        nc.scalar.copy(posT[:], posT_ps[:, :, 0])
+        posb_ps = psum.tile([P, 4, P], F32, tag="p1", name="posb_ps")
+        for t in range(4):
+            nc.tensor.transpose(posb_ps[:, t, :], posT[:, t : t + 1].to_broadcast([P, P]), ident[:])
+        posb = keep.tile([P, 4, P], F32, name="posb")
+        nc.scalar.copy(posb[:], posb_ps[:])
+
+        vs_g = keep.tile([P, N], F32, name="vs_g")
+        nc.vector.tensor_copy(vs_g[:], vs_raw[:].indirect(offsets[:]))
+        vsT_ps = psum.tile([P, 4, P], F32, tag="v0", name="vsT_ps")
+        for t in range(4):
+            nc.tensor.transpose(vsT_ps[:, t, :], vs_g[:, t::4], ident[:])
+        vsT = keep.tile([P, 4], F32, name="vsT")
+        nc.scalar.copy(vsT[:], vsT_ps[:, :, 0])
+
+        q_in = [keep.tile([P, P, 4], BF16, align_bytes=64, name=f"q_in{b}") for b in range(QB)]
+        q_codes = [keep.tile([P, P], U32, align_bytes=64, name=f"q_codes{b}") for b in range(QB)]
+        q_scales = [keep.tile([P, P], U8, align_bytes=64, name=f"q_scales{b}") for b in range(QB)]
+        k_codes = keep.tile([P, N], U32, align_bytes=64, name="k_codes")
+        k_scales = keep.tile([P, N], U8, align_bytes=64, name="k_scales")
+        nc.vector.tensor_copy(k_bf[:, :, 2], k_raw[2][:].indirect(offsets[:]))
+        H = N // 2
+        for h in range(2):
+            nc.vector.tensor_copy(
+                k_bf[:, h * H : (h + 1) * H, 3], k_raw[3][:].indirect(offsets[:, h * H // 16 : (h + 1) * H // 16])
+            )
+        for b in range(QB):
+            nc.scalar.copy(q_in[b][:], q_raw[:, :, b * P : (b + 1) * P].rearrange("p t n -> p n t"))
+        for h in range(2):
+            ks = slice(h * H, (h + 1) * H)
+            nc.vector.quantize_mx(
+                out=k_codes[:, ks].bitcast(FP8X4),
+                scales=k_scales[:, ks],
+                in_=k_bf[:, ks, :].rearrange("p n t -> p (n t)"),
+            )
+        for b in range(QB):
+            nc.vector.quantize_mx(out=q_codes[b][:].bitcast(FP8X4), scales=q_scales[b][:], in_=q_in[b][:].rearrange("p n t -> p (n t)"))
+
+        scores = [[psum.tile([P, H], F32, tag=f"s{b}{h}", name=f"scores{b}{h}") for h in range(2)] for b in range(QB)]
+        for b in range(QB):
+            for h in range(2):
+                ks = slice(h * H, (h + 1) * H)
+                nc.tensor.matmul_mx(
+                    out=scores[b][h][:],
+                    lhsT=q_codes[b][:].bitcast(FP8X4),
+                    lhsT_scale=q_scales[b][:],
+                    rhs=k_codes[:, ks].bitcast(FP8X4),
+                    rhs_scale=k_scales[:, ks],
+                    start=True,
+                    stop=True,
+                )
+
+        v_bf = [keep.tile([P, 4, P], BF16, name=f"v_bf{b}") for b in range(VB)]
+        v_in = keep.tile([P, DV, 4], BF16, align_bytes=64, name="v_in")
+        v_codes = keep.tile([P, DV], U32, align_bytes=64, name="v_codes")
+        v_scales = keep.tile([P, DV], U8, align_bytes=64, name="v_scales")
+
+        def gather_values(b):
+            nc.vector.tensor_copy(v_bf[b][:].rearrange("p t m -> p m t"), v_raw[b][:].indirect(offsets[:]))
+
+        def turn_values(b):
+            ps = psum.tile([P, 4, P], BF16, tag=f"v{b}", name=f"v_ps{b}")
+            for t in range(4):
+                nc.tensor.transpose(ps[:, t, :], v_bf[b][:, t, :], ident_bf[:])
+            nc.scalar.copy(v_in[:, b * P : (b + 1) * P, :], ps[:].rearrange("m t e -> m e t"))
+
+        neg_max = [keep.tile([P, 1], F32, name=f"neg_max{b}") for b in range(QB)]
+        total = [keep.tile([P, 1], F32, name=f"total{b}") for b in range(QB)]
+        inv = [keep.tile([P, 1], F32, name=f"inv{b}") for b in range(QB)]
+        p = [keep.tile([P, N + 4], F32, name=f"p{b}") for b in range(QB)]
+        w_in = [keep.tile([P, P, 4], BF16, align_bytes=64, name=f"w_in{b}") for b in range(QB)]
+        w_codes = [keep.tile([P, P], U32, align_bytes=64, name=f"w_codes{b}") for b in range(QB)]
+        w_scales = [keep.tile([P, P], U8, align_bytes=64, name=f"w_scales{b}") for b in range(QB)]
+        y_sb = [keep.tile([P, DV], F32, name=f"y_sb{b}") for b in range(QB)]
+
+        def add_bias(b):
+            for h in range(2):
+                ms = slice(h * P // 2, (h + 1) * P // 2)
+                nc.vector.scalar_tensor_tensor(
+                    s[b][:, 0:N].rearrange("q (t m) -> q t m", t=4)[:, :, ms],
+                    posb[:, :, ms],
+                    slope_col[:, b : b + 1],
+                    scores[b][h][:].rearrange("q (m t) -> q t m", t=4),
+                    ALU.mult,
+                    ALU.add,
+                )
+
+        def softmax(b):
+            nc.vector.tensor_reduce(neg_max[b][:], s[b][:, 0 : N + 1], mybir.AxisListType.X, ALU.max, negate=True)
+            nc.scalar.activation(p[b][:, 0 : N + 1], s[b][:, 0 : N + 1], ACT.Exp, bias=neg_max[b][:], accum_out=total[b][:])
+
+        def turn_weights(b):
+            ps = psum.tile([P, 4, P], F32, tag=f"p{b}", name=f"p_ps{b}")
+            for t in range(4):
+                nc.tensor.transpose(ps[:, t, :], p[b][:, t * P : (t + 1) * P], ident[:])
+            nc.vector.tensor_tensor(
+                w_in[b][:],
+                ps[:].rearrange("m t q -> m q t"),
+                vsT[:].unsqueeze(1).to_broadcast([P, P, 4]),
+                ALU.mult,
+            )
+
+        def quantise_weights(b):
+            nc.vector.quantize_mx(out=w_codes[b][:].bitcast(FP8X4), scales=w_scales[b][:], in_=w_in[b][:].rearrange("m q t -> m (q t)"))
+
+        def quantise_values(b):
+            es = slice(b * P, (b + 1) * P)
+            nc.vector.quantize_mx(out=v_codes[:, es].bitcast(FP8X4), scales=v_scales[:, es], in_=v_in[:, es, :].rearrange("m e t -> m (e t)"))
+
+        y = [[psum.tile([P, P], F32, tag=f"s{b}{v}", name=f"y{b}{v}") for v in range(VB)] for b in range(QB)]
+
+        def product(b, v):
+            es = slice(v * P, (v + 1) * P)
+            nc.tensor.matmul_mx(
+                out=y[b][v][:],
+                lhsT=w_codes[b][:].bitcast(FP8X4),
+                lhsT_scale=w_scales[b][:],
+                rhs=v_codes[:, es].bitcast(FP8X4),
+                rhs_scale=v_scales[:, es],
+                start=True,
+                stop=True,
+            )
+
+        def finish(b):
+            for v in range(VB):
+                es = slice(v * P, (v + 1) * P)
+                if b == 0 or v == 0:
+                    nc.scalar.activation(y_sb[b][:, es], y[b][v][:], ACT.Copy, scale=inv[b][:])
+                else:
+                    nc.vector.tensor_scalar(y_sb[b][:, es], y[b][v][:], inv[b][:], None, ALU.mult)
+            nc.sync.dma_start(out[0, b * P : (b + 1) * P, :], y_sb[b][:])
+
+        add_bias(0)
+        add_bias(1)
+        softmax(0)
+        softmax(1)
+        for b in range(QB):
+            nc.vector.reciprocal(inv[b][:], total[b][:])
+        gather_values(0)
+        turn_values(0)
+        gather_values(1)
+        turn_weights(0)
+        turn_values(1)
+        turn_weights(1)
+        quantise_values(0)
+        quantise_weights(0)
+        product(0, 0)
+        quantise_weights(1)
+        product(1, 0)
+        quantise_values(1)
+        product(0, 1)
+        product(1, 1)
+        finish(0)
+        finish(1)

@@ -16,6 +16,7 @@ P = 128
 D, NQ, N, T, DV = 512, 256, 512, 2048, 256
 QB = NQ // P
 VB = DV // P
+R0 = P - 4
 FLOPS = 2 * NQ * N * (D + DV)
 BYTES = 4 * (D * NQ + D * T + DV * T + 2 * T + 2 * NQ + NQ * DV) + 2 * P * (N // 16)
 
@@ -36,20 +37,19 @@ def tile_attend_x_alibi_sink_srt_kernel(tc, qT, kT, vT, vs, pos, slope, sink, of
         k_planes = kT.rearrange("(p t) n -> p t n", t=4)
         nc.sync.dma_start(k_raw[0][:], k_planes[:, 0, :])
         nc.sync.dma_start(offsets[:], offs)
-        nc.sync.dma_start(k_raw[1][:], k_planes[:, 1, :])
 
         warm = keep.tile([P, 1], F32, name="warm")
         nc.vector.memset(warm[:], 0.0)
         nc.scalar.activation(warm[:], warm[:], ACT.Exp)
 
-        nc.vector.memset(rows[:], 0.0)
-        nc.sync.dma_start(rows[0:2, :], slope.rearrange("o (b p) x -> (o b) (p x)", p=P))
-        nc.sync.dma_start(rows[2:4, :], sink.rearrange("o (b p) x -> (o b) (p x)", p=P))
-        nc.vector.memset(pos_raw[:], 0.0)
-        nc.sync.dma_start(pos_raw[0:1, :], pos[0:1, :])
-        nc.vector.memset(vs_raw[:], 0.0)
-        nc.sync.dma_start(vs_raw[0:1, :], vs[0:1, :])
-        for t in (2, 3):
+        nc.sync.dma_start(pos_raw[P - 1 : P, :], pos[0:1, :])
+        nc.sync.dma_start(vs_raw[P - 1 : P, :], vs[0:1, :])
+        nc.sync.dma_start(rows[R0 : R0 + 2, :], slope.rearrange("o (b p) x -> (o b) (p x)", p=P))
+        nc.sync.dma_start(rows[R0 + 2 : R0 + 4, :], sink.rearrange("o (b p) x -> (o b) (p x)", p=P))
+        nc.vector.memset(pos_raw[0 : P - 1, :], 0.0)
+        nc.vector.memset(rows[0:R0, :], 0.0)
+        nc.vector.memset(vs_raw[0 : P - 1, :], 0.0)
+        for t in (1, 2, 3):
             nc.sync.dma_start(k_raw[t][:], k_planes[:, t, :])
         nc.sync.dma_start(q_raw[:], qT.rearrange("o (p t) n -> p (o t) n", t=4))
         for b in range(VB):
@@ -68,9 +68,9 @@ def tile_attend_x_alibi_sink_srt_kernel(tc, qT, kT, vT, vs, pos, slope, sink, of
         cols_ps = psum.tile([P, P], F32, tag="s00", name="cols_ps")
         nc.tensor.transpose(cols_ps[:], rows[:], ident[:])
         slope_col = keep.tile([P, QB], F32, name="slope_col")
-        nc.scalar.copy(slope_col[:], cols_ps[:, 0:QB])
+        nc.scalar.copy(slope_col[:], cols_ps[:, R0 : R0 + QB])
         for b in range(QB):
-            nc.scalar.copy(s[b][:, N : N + 1], cols_ps[:, QB + b : QB + b + 1])
+            nc.scalar.copy(s[b][:, N : N + 1], cols_ps[:, R0 + QB + b : R0 + QB + b + 1])
 
         pos_g = keep.tile([P, N], F32, name="pos_g")
         nc.vector.tensor_copy(pos_g[:], pos_raw[:].indirect(offsets[:]))
@@ -78,7 +78,7 @@ def tile_attend_x_alibi_sink_srt_kernel(tc, qT, kT, vT, vs, pos, slope, sink, of
         for t in range(4):
             nc.tensor.transpose(posT_ps[:, t, :], pos_g[:, t::4], ident[:])
         posT = keep.tile([P, 4], F32, name="posT")
-        nc.scalar.copy(posT[:], posT_ps[:, :, 0])
+        nc.scalar.copy(posT[:], posT_ps[:, :, P - 1])
         posb_ps = psum.tile([P, 4, P], F32, tag="p1", name="posb_ps")
         for t in range(4):
             nc.tensor.transpose(posb_ps[:, t, :], posT[:, t : t + 1].to_broadcast([P, P]), ident[:])
@@ -91,7 +91,7 @@ def tile_attend_x_alibi_sink_srt_kernel(tc, qT, kT, vT, vs, pos, slope, sink, of
         for t in range(4):
             nc.tensor.transpose(vsT_ps[:, t, :], vs_g[:, t::4], ident[:])
         vsT = keep.tile([P, 4], F32, name="vsT")
-        nc.scalar.copy(vsT[:], vsT_ps[:, :, 0])
+        nc.scalar.copy(vsT[:], vsT_ps[:, :, P - 1])
 
         q_in = [keep.tile([P, P, 4], BF16, align_bytes=64, name=f"q_in{b}") for b in range(QB)]
         q_codes = [keep.tile([P, P], U32, align_bytes=64, name=f"q_codes{b}") for b in range(QB)]

@@ -57,8 +57,6 @@ def tile_attend_x_alibi_sink_srt_kernel(tc, qT, kT, vT, vs, pos, slope, sink, of
 
         ident = keep.tile([P, P], F32, name="ident")
         make_identity(nc, ident[:])
-        ident_bf = keep.tile([P, P], BF16, name="ident_bf")
-        nc.gpsimd.tensor_copy(ident_bf[:], ident[:])
 
         k_bf = keep.tile([P, N, 4], BF16, align_bytes=64, name="k_bf")
         for t in (0, 1):
@@ -130,19 +128,20 @@ def tile_attend_x_alibi_sink_srt_kernel(tc, qT, kT, vT, vs, pos, slope, sink, of
                     stop=True,
                 )
 
-        v_bf = [keep.tile([P, 4, P], BF16, name=f"v_bf{b}") for b in range(VB)]
-        v_in = keep.tile([P, DV, 4], BF16, align_bytes=64, name="v_in")
+        v_bf = [keep.tile([P, N], BF16, name=f"v_bf{b}") for b in range(VB)]
+        v_in = [keep.tile([P, 4 * P], BF16, align_bytes=64, name=f"v_in{b}") for b in range(VB)]
         v_codes = keep.tile([P, DV], U32, align_bytes=64, name="v_codes")
         v_scales = keep.tile([P, DV], U8, align_bytes=64, name="v_scales")
 
         def gather_values(b):
-            nc.vector.tensor_copy(v_bf[b][:].rearrange("p t m -> p m t"), v_raw[b][:].indirect(offsets[:]))
+            nc.vector.tensor_copy(v_bf[b][:], v_raw[b][:].indirect(offsets[:]))
 
         def turn_values(b):
-            ps = psum.tile([P, 4, P], BF16, tag=f"v{b}", name=f"v_ps{b}")
-            for t in range(4):
-                nc.tensor.transpose(ps[:, t, :], v_bf[b][:, t, :], ident_bf[:])
-            nc.scalar.copy(v_in[:, b * P : (b + 1) * P, :], ps[:].rearrange("m t e -> m e t"))
+            ps = psum.tile([P, 2, P], F32, tag=f"v{b}", name=f"v_ps{b}")
+            words = v_bf[b][:].bitcast(F32)
+            for u in range(2):
+                nc.tensor.transpose(ps[:, u, :], words[:, u::2], ident[:])
+            nc.scalar.copy(v_in[b][:].bitcast(F32).rearrange("m (e u) -> m e u", u=2), ps[:].rearrange("m u e -> m e u"))
 
         neg_max = [keep.tile([P, 1], F32, name=f"neg_max{b}") for b in range(QB)]
         total = [keep.tile([P, 1], F32, name=f"total{b}") for b in range(QB)]
@@ -185,7 +184,7 @@ def tile_attend_x_alibi_sink_srt_kernel(tc, qT, kT, vT, vs, pos, slope, sink, of
 
         def quantise_values(b):
             es = slice(b * P, (b + 1) * P)
-            nc.vector.quantize_mx(out=v_codes[:, es].bitcast(FP8X4), scales=v_scales[:, es], in_=v_in[:, es, :].rearrange("m e t -> m (e t)"))
+            nc.vector.quantize_mx(out=v_codes[:, es].bitcast(FP8X4), scales=v_scales[:, es], in_=v_in[b][:])
 
         y = [[psum.tile([P, P], F32, tag=f"s{b}{v}", name=f"y{b}{v}") for v in range(VB)] for b in range(QB)]
 

@@ -17,6 +17,7 @@ D, NQ, N, T, DV = 512, 256, 512, 2048, 256
 QB = NQ // P
 VB = DV // P
 R0 = P - 4
+KIB = 1024
 FLOPS = 2 * NQ * N * (D + DV)
 BYTES = 4 * (D * NQ + D * T + DV * T + 2 * T + 2 * NQ + NQ * DV) + 2 * P * (N // 16)
 
@@ -25,12 +26,13 @@ def tile_attend_x_alibi_sink_srt_kernel(tc, qT, kT, vT, vs, pos, slope, sink, of
     nc = tc.nc
     with ExitStack() as ctx:
         keep = ctx.enter_context(tc.tile_pool(name="keep", bufs=1))
+        late = ctx.enter_context(tc.tile_pool(name="late", bufs=1))
         psum = ctx.enter_context(tc.psum_pool(name="psum", bufs=1))
 
         offsets = keep.tile([P, N // 16], U16, name="offsets")
         k_raw = [keep.tile([P, T], F32, name=f"k_raw{t}") for t in range(4)]
         q_raw = keep.tile([P, 4, NQ], F32, name="q_raw")
-        v_raw = [keep.tile([P, T], F32, name=f"v_raw{b}") for b in range(VB)]
+        v_raw = [keep.tile([P, T], F32, name="v_raw0"), late.tile([P, T], F32, offset=8 * KIB, name="v_raw1")]
         rows = keep.tile([P, P], F32, name="rows")
         pos_raw = keep.tile([P, T], F32, name="pos_raw")
         vs_raw = keep.tile([P, T], F32, name="vs_raw")
@@ -62,7 +64,7 @@ def tile_attend_x_alibi_sink_srt_kernel(tc, qT, kT, vT, vs, pos, slope, sink, of
         for t in (0, 1):
             nc.vector.tensor_copy(k_bf[:, :, t], k_raw[t][:].indirect(offsets[:]))
 
-        s = [keep.tile([P, N + 4], F32, name=f"s{b}") for b in range(QB)]
+        s = [late.tile([P, N + 4], F32, align_bytes=64, offset=4 * KIB * b, name=f"s{b}") for b in range(QB)]
         cols_ps = psum.tile([P, P], F32, tag="s00", name="cols_ps")
         nc.tensor.transpose(cols_ps[:], rows[:], ident[:])
         slope_col = keep.tile([P, QB], F32, name="slope_col")
@@ -80,16 +82,14 @@ def tile_attend_x_alibi_sink_srt_kernel(tc, qT, kT, vT, vs, pos, slope, sink, of
         posb_ps = psum.tile([P, 4, P], F32, tag="p1", name="posb_ps")
         for t in range(4):
             nc.tensor.transpose(posb_ps[:, t, :], posT[:, t : t + 1].to_broadcast([P, P]), ident[:])
-        posb = keep.tile([P, 4, P], F32, name="posb")
+        posb = keep.tile([P, 4, P], F32, tag="posb", name="posb")
         nc.scalar.copy(posb[:], posb_ps[:])
 
         vs_g = keep.tile([P, N], F32, name="vs_g")
         nc.vector.tensor_copy(vs_g[:], vs_raw[:].indirect(offsets[:]))
-        vsT_ps = psum.tile([P, 4, P], F32, tag="v0", name="vsT_ps")
+        vsT_ps = [psum.tile([P, 2, P], F32, tag=f"v{u}", name=f"vsT_ps{u}") for u in range(2)]
         for t in range(4):
-            nc.tensor.transpose(vsT_ps[:, t, :], vs_g[:, t::4], ident[:])
-        vsT = keep.tile([P, 4], F32, name="vsT")
-        nc.scalar.copy(vsT[:], vsT_ps[:, :, P - 1])
+            nc.tensor.transpose(vsT_ps[t // 2][:, t % 2, :], vs_g[:, t::4], ident[:])
 
         q_in = [keep.tile([P, P, 4], BF16, align_bytes=64, name=f"q_in{b}") for b in range(QB)]
         q_codes = [keep.tile([P, P], U32, align_bytes=64, name=f"q_codes{b}") for b in range(QB)]
@@ -103,7 +103,10 @@ def tile_attend_x_alibi_sink_srt_kernel(tc, qT, kT, vT, vs, pos, slope, sink, of
                 k_bf[:, h * H : (h + 1) * H, 3], k_raw[3][:].indirect(offsets[:, h * H // 16 : (h + 1) * H // 16])
             )
         for b in range(QB):
-            nc.scalar.copy(q_in[b][:], q_raw[:, :, b * P : (b + 1) * P].rearrange("p t n -> p n t"))
+            nc.scalar.copy(
+                q_in[b][:].rearrange("p (c i) t -> p c t i", i=4),
+                q_raw[:, :, b * P : (b + 1) * P].rearrange("p t (c i) -> p c t i", i=4),
+            )
         for h in range(2):
             ks = slice(h * H, (h + 1) * H)
             nc.vector.quantize_mx(
@@ -128,29 +131,31 @@ def tile_attend_x_alibi_sink_srt_kernel(tc, qT, kT, vT, vs, pos, slope, sink, of
                     stop=True,
                 )
 
-        v_bf = [keep.tile([P, N], BF16, name=f"v_bf{b}") for b in range(VB)]
+        v_all = keep.tile([P, VB * N], BF16, tag="posb", name="v_all")
+        v_bf = [v_all[:, b * N : (b + 1) * N] for b in range(VB)]
         v_in = [keep.tile([P, 4 * P], BF16, align_bytes=64, name=f"v_in{b}") for b in range(VB)]
-        v_codes = keep.tile([P, DV], U32, align_bytes=64, name="v_codes")
+        v_codes = late.tile([P, DV], U32, align_bytes=64, offset=8 * KIB, name="v_codes")
         v_scales = keep.tile([P, DV], U8, align_bytes=64, name="v_scales")
 
         def gather_values(b):
-            nc.vector.tensor_copy(v_bf[b][:], v_raw[b][:].indirect(offsets[:]))
+            nc.vector.tensor_copy(v_bf[b], v_raw[b][:].indirect(offsets[:]))
 
         def turn_values(b):
             ps = psum.tile([P, 2, P], F32, tag=f"v{b}", name=f"v_ps{b}")
-            words = v_bf[b][:].bitcast(F32)
+            words = v_bf[b].bitcast(F32)
             for u in range(2):
                 nc.tensor.transpose(ps[:, u, :], words[:, u::2], ident[:])
             nc.scalar.copy(v_in[b][:].bitcast(F32).rearrange("m (e u) -> m e u", u=2), ps[:].rearrange("m u e -> m e u"))
 
         neg_max = [keep.tile([P, 1], F32, name=f"neg_max{b}") for b in range(QB)]
-        total = [keep.tile([P, 1], F32, name=f"total{b}") for b in range(QB)]
-        inv = [keep.tile([P, 1], F32, name=f"inv{b}") for b in range(QB)]
+        total = keep.tile([P, QB], F32, name="total")
+        inv = keep.tile([P, QB], F32, name="inv")
+        vsT = late.tile([P, 4], F32, offset=4 * KIB, name="vsT")
         p = [keep.tile([P, N + 4], F32, name=f"p{b}") for b in range(QB)]
-        w_in = [keep.tile([P, P, 4], BF16, align_bytes=64, name=f"w_in{b}") for b in range(QB)]
+        w_in = [late.tile([P, P, 4], BF16, align_bytes=64, offset=(9 + b) * KIB, name=f"w_in{b}") for b in range(QB)]
         w_codes = [keep.tile([P, P], U32, align_bytes=64, name=f"w_codes{b}") for b in range(QB)]
         w_scales = [keep.tile([P, P], U8, align_bytes=64, name=f"w_scales{b}") for b in range(QB)]
-        y_sb = [keep.tile([P, DV], F32, name=f"y_sb{b}") for b in range(QB)]
+        y_sb = [keep.tile([P, QB, P], F32, name=f"y_sb{v}") for v in range(VB)]
 
         def add_bias(b):
             for h in range(2):
@@ -166,7 +171,7 @@ def tile_attend_x_alibi_sink_srt_kernel(tc, qT, kT, vT, vs, pos, slope, sink, of
 
         def softmax(b):
             nc.vector.tensor_reduce(neg_max[b][:], s[b][:, 0 : N + 1], mybir.AxisListType.X, ALU.max, negate=True)
-            nc.scalar.activation(p[b][:, 0 : N + 1], s[b][:, 0 : N + 1], ACT.Exp, bias=neg_max[b][:], accum_out=total[b][:])
+            nc.scalar.activation(p[b][:, 0 : N + 1], s[b][:, 0 : N + 1], ACT.Exp, bias=neg_max[b][:], accum_out=total[:, b : b + 1])
 
         def turn_weights(b):
             ps = psum.tile([P, 4, P], F32, tag=f"p{b}", name=f"p_ps{b}")
@@ -200,30 +205,30 @@ def tile_attend_x_alibi_sink_srt_kernel(tc, qT, kT, vT, vs, pos, slope, sink, of
                 stop=True,
             )
 
-        def finish(b):
-            for v in range(VB):
-                es = slice(v * P, (v + 1) * P)
+        def finish(v):
+            for b in range(QB):
                 if b == 0 or v == 0:
-                    nc.scalar.activation(y_sb[b][:, es], y[b][v][:], ACT.Copy, scale=inv[b][:])
+                    nc.scalar.activation(y_sb[v][:, b, :], y[b][v][:], ACT.Copy, scale=inv[:, b : b + 1])
                 else:
-                    nc.vector.tensor_scalar(y_sb[b][:, es], y[b][v][:], inv[b][:], None, ALU.mult)
-            nc.sync.dma_start(out[0, b * P : (b + 1) * P, :], y_sb[b][:])
+                    nc.vector.tensor_scalar(y_sb[v][:, b, :], y[b][v][:], inv[:, b : b + 1], None, ALU.mult)
+            nc.sync.dma_start(out.rearrange("o (b q) e -> q (o b) e", q=P)[:, :, v * P : (v + 1) * P], y_sb[v][:])
 
         add_bias(0)
         add_bias(1)
         softmax(0)
         softmax(1)
-        for b in range(QB):
-            nc.vector.reciprocal(inv[b][:], total[b][:])
+        for u in range(2):
+            nc.scalar.copy(vsT[:, 2 * u : 2 * u + 2], vsT_ps[u][:, :, P - 1])
         gather_values(0)
-        turn_values(0)
         gather_values(1)
         turn_weights(0)
-        turn_values(1)
         turn_weights(1)
+        turn_values(0)
+        turn_values(1)
         quantise_values(0)
         quantise_weights(0)
         product(0, 0)
+        nc.vector.reciprocal(inv[:], total[:])
         quantise_weights(1)
         product(1, 0)
         quantise_values(1)

@@ -37,21 +37,26 @@ def tile_attend_x_alibi_sink_srt_kernel(tc, qT, kT, vT, vs, pos, slope, sink, of
         pos_raw = keep.tile([P, T], F32, name="pos_raw")
         vs_raw = keep.tile([P, T], F32, name="vs_raw")
         k_planes = kT.rearrange("(p t) n -> p t n", t=4)
-        nc.sync.dma_start(k_raw[0][:], k_planes[:, 0, :])
         nc.sync.dma_start(offsets[:], offs)
+        nc.sync.dma_start(pos_raw[P - 1 : P, :], pos[0:1, :])
+        nc.sync.dma_start(vs_raw[P - 1 : P, :], vs[0:1, :])
+        for t in (0, 1):
+            nc.sync.dma_start(k_raw[t][:], k_planes[:, t, :])
+        nc.sync.dma_start(rows[R0 : R0 + 2, :], slope.rearrange("o (b p) x -> (o b) (p x)", p=P))
+        nc.sync.dma_start(rows[R0 + 2 : R0 + 4, :], sink.rearrange("o (b p) x -> (o b) (p x)", p=P))
 
         warm = keep.tile([P, 1], F32, name="warm")
         nc.vector.memset(warm[:], 0.0)
         nc.scalar.activation(warm[:], warm[:], ACT.Exp)
 
-        nc.sync.dma_start(pos_raw[P - 1 : P, :], pos[0:1, :])
-        nc.sync.dma_start(vs_raw[P - 1 : P, :], vs[0:1, :])
-        nc.sync.dma_start(rows[R0 : R0 + 2, :], slope.rearrange("o (b p) x -> (o b) (p x)", p=P))
-        nc.sync.dma_start(rows[R0 + 2 : R0 + 4, :], sink.rearrange("o (b p) x -> (o b) (p x)", p=P))
         nc.vector.memset(pos_raw[0 : P - 1, :], 0.0)
-        nc.vector.memset(rows[0:R0, :], 0.0)
         nc.vector.memset(vs_raw[0 : P - 1, :], 0.0)
-        for t in (1, 2, 3):
+        nc.vector.memset(rows[0:R0, :], 0.0)
+        pos_g = keep.tile([P, N], F32, name="pos_g")
+        nc.vector.tensor_copy(pos_g[:], pos_raw[:].indirect(offsets[:]))
+        vs_g = keep.tile([P, N], F32, name="vs_g")
+        nc.vector.tensor_copy(vs_g[:], vs_raw[:].indirect(offsets[:]))
+        for t in (2, 3):
             nc.sync.dma_start(k_raw[t][:], k_planes[:, t, :])
         nc.sync.dma_start(q_raw[:], qT.rearrange("o (p t) n -> p (o t) n", t=4))
         for b in range(VB):
@@ -72,8 +77,6 @@ def tile_attend_x_alibi_sink_srt_kernel(tc, qT, kT, vT, vs, pos, slope, sink, of
         for b in range(QB):
             nc.scalar.copy(s[b][:, N : N + 1], cols_ps[:, R0 + QB + b : R0 + QB + b + 1])
 
-        pos_g = keep.tile([P, N], F32, name="pos_g")
-        nc.vector.tensor_copy(pos_g[:], pos_raw[:].indirect(offsets[:]))
         posT_ps = psum.tile([P, 4, P], F32, tag="p0", name="posT_ps")
         for t in range(4):
             nc.tensor.transpose(posT_ps[:, t, :], pos_g[:, t::4], ident[:])
@@ -85,8 +88,6 @@ def tile_attend_x_alibi_sink_srt_kernel(tc, qT, kT, vT, vs, pos, slope, sink, of
         posb = keep.tile([P, 4, P], F32, tag="posb", name="posb")
         nc.scalar.copy(posb[:], posb_ps[:])
 
-        vs_g = keep.tile([P, N], F32, name="vs_g")
-        nc.vector.tensor_copy(vs_g[:], vs_raw[:].indirect(offsets[:]))
         vsT_ps = [psum.tile([P, 2, P], F32, tag=f"v{u}", name=f"vsT_ps{u}") for u in range(2)]
         for t in range(4):
             nc.tensor.transpose(vsT_ps[t // 2][:, t % 2, :], vs_g[:, t::4], ident[:])

@@ -66,8 +66,10 @@ def tile_attend_x_alibi_sink_srt_kernel(tc, qT, kT, vT, vs, pos, slope, sink, of
         make_identity(nc, ident[:])
 
         k_bf = keep.tile([P, N, 4], BF16, align_bytes=64, name="k_bf")
+        k_pair = keep.tile([P, 2, N], BF16, name="k_pair")
         for t in (0, 1):
-            nc.vector.tensor_copy(k_bf[:, :, t], k_raw[t][:].indirect(offsets[:]))
+            nc.vector.tensor_copy(k_pair[:, t, :], k_raw[t][:].indirect(offsets[:]))
+        nc.scalar.copy(k_bf[:, :, 0:2], k_pair[:].rearrange("p t n -> p n t"))
 
         s = [late.tile([P, N + 4], F32, align_bytes=64, offset=4 * KIB * b, name=f"s{b}") for b in range(QB)]
         cols_ps = psum.tile([P, P], F32, tag="s00", name="cols_ps")
@@ -153,7 +155,7 @@ def tile_attend_x_alibi_sink_srt_kernel(tc, qT, kT, vT, vs, pos, slope, sink, of
         inv = keep.tile([P, QB], F32, name="inv")
         vsT = late.tile([P, 4], F32, offset=4 * KIB, name="vsT")
         p = [keep.tile([P, N + 4], F32, name=f"p{b}") for b in range(QB)]
-        w_in = [late.tile([P, P, 4], BF16, align_bytes=64, offset=(9 + b) * KIB, name=f"w_in{b}") for b in range(QB)]
+        w_in = [keep.tile([P, P, 4], BF16, align_bytes=64, name="w_in0"), late.tile([P, P, 4], BF16, align_bytes=64, offset=10 * KIB, name="w_in1")]
         w_codes = [keep.tile([P, P], U32, align_bytes=64, name=f"w_codes{b}") for b in range(QB)]
         w_scales = [keep.tile([P, P], U8, align_bytes=64, name=f"w_scales{b}") for b in range(QB)]
         y_sb = [keep.tile([P, QB, P], F32, name=f"y_sb{v}") for v in range(VB)]
@@ -178,6 +180,15 @@ def tile_attend_x_alibi_sink_srt_kernel(tc, qT, kT, vT, vs, pos, slope, sink, of
             ps = psum.tile([P, 4, P], F32, tag=f"p{b}", name=f"p_ps{b}")
             for t in range(4):
                 nc.tensor.transpose(ps[:, t, :], p[b][:, t * P : (t + 1) * P], ident[:])
+            if b == 0:
+                lanes = keep.tile([P, 4, P], BF16, name="lanes")
+                for t in range(4):
+                    nc.scalar.activation(lanes[:, t, :], ps[:, t, :], ACT.Copy, scale=vsT[:, t : t + 1])
+                nc.scalar.copy(
+                    w_in[b][:].rearrange("m (c i) t -> m c t i", i=4),
+                    lanes[:].rearrange("m t (c i) -> m c t i", i=4),
+                )
+                return
             nc.vector.tensor_tensor(
                 w_in[b][:],
                 ps[:].rearrange("m t q -> m q t"),
@@ -226,12 +237,12 @@ def tile_attend_x_alibi_sink_srt_kernel(tc, qT, kT, vT, vs, pos, slope, sink, of
         turn_weights(1)
         turn_values(0)
         turn_values(1)
-        quantise_values(0)
-        quantise_weights(0)
-        product(0, 0)
         nc.vector.reciprocal(inv[:], total[:])
         quantise_weights(1)
+        quantise_weights(0)
+        quantise_values(0)
         product(1, 0)
+        product(0, 0)
         quantise_values(1)
         product(0, 1)
         product(1, 1)

@@ -34,12 +34,12 @@ def tile_attend_x_alibi_sink_srt_kernel(tc, qT, kT, vT, vs, pos, slope, sink, of
         q_raw = keep.tile([P, 4, NQ], F32, name="q_raw")
         v_raw = [keep.tile([P, T], F32, name="v_raw0"), late.tile([P, T], F32, offset=8 * KIB, name="v_raw1")]
         rows = keep.tile([P, P], F32, name="rows")
-        pos_raw = keep.tile([P, T], F32, name="pos_raw")
-        vs_raw = keep.tile([P, T], F32, name="vs_raw")
+        pos_raw = late.tile([P, T], F32, offset=16 * KIB, name="pos_raw")
+        vs_raw = late.tile([P, T], F32, offset=24 * KIB, name="vs_raw")
         k_planes = kT.rearrange("(p t) n -> p t n", t=4)
         nc.sync.dma_start(offsets[:], offs)
-        nc.sync.dma_start(pos_raw[P - 1 : P, :], pos[0:1, :])
-        nc.sync.dma_start(vs_raw[P - 1 : P, :], vs[0:1, :])
+        nc.scalar.dma_start(pos_raw[P - 1 : P, :], pos[0:1, :])
+        nc.scalar.dma_start(vs_raw[P - 1 : P, :], vs[0:1, :])
         for t in (0, 1):
             nc.sync.dma_start(k_raw[t][:], k_planes[:, t, :])
         nc.sync.dma_start(rows[R0 : R0 + 2, :], slope.rearrange("o (b p) x -> (o b) (p x)", p=P))
@@ -66,7 +66,7 @@ def tile_attend_x_alibi_sink_srt_kernel(tc, qT, kT, vT, vs, pos, slope, sink, of
         make_identity(nc, ident[:])
 
         k_bf = keep.tile([P, N, 4], BF16, align_bytes=64, name="k_bf")
-        k_pair = keep.tile([P, 2, N], BF16, name="k_pair")
+        k_pair = late.tile([P, 2, N], BF16, offset=23 * KIB, name="k_pair")
         for t in (0, 1):
             nc.vector.tensor_copy(k_pair[:, t, :], k_raw[t][:].indirect(offsets[:]))
         nc.scalar.copy(k_bf[:, :, 0:2], k_pair[:].rearrange("p t n -> p n t"))

@@ -33,7 +33,7 @@ def tile_attend_x_alibi_sink_srt_kernel(tc, qT, kT, vT, vs, pos, slope, sink, of
         k_raw = [keep.tile([P, T], F32, name=f"k_raw{t}") for t in range(4)]
         q_raw = keep.tile([P, 4, NQ], F32, name="q_raw")
         v_raw = [keep.tile([P, T], F32, name="v_raw0"), late.tile([P, T], F32, offset=8 * KIB, name="v_raw1")]
-        rows = keep.tile([P, P], F32, name="rows")
+        rows = keep.tile([P, P], F32, align_bytes=64, tag="rows", name="rows")
         pos_raw = late.tile([P, T], F32, offset=16 * KIB, name="pos_raw")
         vs_raw = late.tile([P, T], F32, offset=24 * KIB, name="vs_raw")
         k_planes = kT.rearrange("(p t) n -> p t n", t=4)
@@ -42,8 +42,6 @@ def tile_attend_x_alibi_sink_srt_kernel(tc, qT, kT, vT, vs, pos, slope, sink, of
         nc.scalar.dma_start(vs_raw[P - 1 : P, :], vs[0:1, :])
         for t in (0, 1):
             nc.sync.dma_start(k_raw[t][:], k_planes[:, t, :])
-        nc.sync.dma_start(rows[R0 : R0 + 2, :], slope.rearrange("o (b p) x -> (o b) (p x)", p=P))
-        nc.sync.dma_start(rows[R0 + 2 : R0 + 4, :], sink.rearrange("o (b p) x -> (o b) (p x)", p=P))
 
         warm = keep.tile([P, 1], F32, name="warm")
         nc.vector.memset(warm[:], 0.0)
@@ -56,8 +54,13 @@ def tile_attend_x_alibi_sink_srt_kernel(tc, qT, kT, vT, vs, pos, slope, sink, of
         nc.vector.tensor_copy(pos_g[:], pos_raw[:].indirect(offsets[:]))
         vs_g = keep.tile([P, N], F32, name="vs_g")
         nc.vector.tensor_copy(vs_g[:], vs_raw[:].indirect(offsets[:]))
-        for t in (2, 3):
-            nc.sync.dma_start(k_raw[t][:], k_planes[:, t, :])
+        H = N // 2
+        PRE = T - H
+        nc.sync.dma_start(k_raw[2][:], k_planes[:, 2, :])
+        nc.sync.dma_start(k_raw[3][:, 0:PRE], k_planes[:, 3, 0:PRE])
+        nc.sync.dma_start(k_raw[3][:, PRE:T], k_planes[:, 3, PRE:T])
+        nc.sync.dma_start(rows[R0 : R0 + 2, :], slope.rearrange("o (b p) x -> (o b) (p x)", p=P))
+        nc.sync.dma_start(rows[R0 + 2 : R0 + 4, :], sink.rearrange("o (b p) x -> (o b) (p x)", p=P))
         nc.sync.dma_start(q_raw[:], qT.rearrange("o (p t) n -> p (o t) n", t=4))
         for b in range(VB):
             nc.sync.dma_start(v_raw[b][:], vT[b * P : (b + 1) * P, :])
@@ -90,21 +93,20 @@ def tile_attend_x_alibi_sink_srt_kernel(tc, qT, kT, vT, vs, pos, slope, sink, of
         posb = keep.tile([P, 4, P], F32, tag="posb", name="posb")
         nc.scalar.copy(posb[:], posb_ps[:])
 
-        vsT_ps = [psum.tile([P, 2, P], F32, tag=f"v{u}", name=f"vsT_ps{u}") for u in range(2)]
+        vsT_ps = psum.tile([P, 4, P], F32, tag="p2", name="vsT_ps")
         for t in range(4):
-            nc.tensor.transpose(vsT_ps[t // 2][:, t % 2, :], vs_g[:, t::4], ident[:])
+            nc.tensor.transpose(vsT_ps[:, t, :], vs_g[:, t::4], ident[:])
+        vsT = keep.tile([P, 4], F32, name="vsT")
+        nc.scalar.copy(vsT[:], vsT_ps[:, :, P - 1])
 
         q_in = [keep.tile([P, P, 4], BF16, align_bytes=64, name=f"q_in{b}") for b in range(QB)]
         q_codes = [keep.tile([P, P], U32, align_bytes=64, name=f"q_codes{b}") for b in range(QB)]
         q_scales = [keep.tile([P, P], U8, align_bytes=64, name=f"q_scales{b}") for b in range(QB)]
         k_codes = keep.tile([P, N], U32, align_bytes=64, name="k_codes")
-        k_scales = keep.tile([P, N], U8, align_bytes=64, name="k_scales")
+        k_scales = keep.tile([P, N], U8, align_bytes=64, tag="rows", name="k_scales")
         nc.vector.tensor_copy(k_bf[:, :, 2], k_raw[2][:].indirect(offsets[:]))
-        H = N // 2
-        for h in range(2):
-            nc.vector.tensor_copy(
-                k_bf[:, h * H : (h + 1) * H, 3], k_raw[3][:].indirect(offsets[:, h * H // 16 : (h + 1) * H // 16])
-            )
+        nc.vector.tensor_copy(k_bf[:, 0:H, 3], k_raw[3][:, 0:PRE].indirect(offsets[:, 0 : H // 16]))
+        nc.vector.tensor_copy(k_bf[:, H:N, 3], k_raw[3][:].indirect(offsets[:, H // 16 : N // 16]))
         for b in range(QB):
             nc.scalar.copy(
                 q_in[b][:].rearrange("p (c i) t -> p c t i", i=4),
@@ -144,7 +146,7 @@ def tile_attend_x_alibi_sink_srt_kernel(tc, qT, kT, vT, vs, pos, slope, sink, of
             nc.vector.tensor_copy(v_bf[b], v_raw[b][:].indirect(offsets[:]))
 
         def turn_values(b):
-            ps = psum.tile([P, 2, P], F32, tag=f"v{b}", name=f"v_ps{b}")
+            ps = psum.tile([P, 2, P], F32, tag=f"p{b}", name=f"v_ps{b}")
             words = v_bf[b].bitcast(F32)
             for u in range(2):
                 nc.tensor.transpose(ps[:, u, :], words[:, u::2], ident[:])
@@ -153,12 +155,13 @@ def tile_attend_x_alibi_sink_srt_kernel(tc, qT, kT, vT, vs, pos, slope, sink, of
         neg_max = [keep.tile([P, 1], F32, name=f"neg_max{b}") for b in range(QB)]
         total = keep.tile([P, QB], F32, name="total")
         inv = keep.tile([P, QB], F32, name="inv")
-        vsT = late.tile([P, 4], F32, offset=4 * KIB, name="vsT")
         p = [keep.tile([P, N + 4], F32, name=f"p{b}") for b in range(QB)]
-        w_in = [keep.tile([P, P, 4], BF16, align_bytes=64, name="w_in0"), late.tile([P, P, 4], BF16, align_bytes=64, offset=10 * KIB, name="w_in1")]
+        w_in = [keep.tile([P, P, 4], BF16, align_bytes=64, name="w_in0"), keep.tile([P, P, 4], BF16, align_bytes=64, name="w_in1")]
         w_codes = [keep.tile([P, P], U32, align_bytes=64, name=f"w_codes{b}") for b in range(QB)]
         w_scales = [keep.tile([P, P], U8, align_bytes=64, name=f"w_scales{b}") for b in range(QB)]
         y_sb = [keep.tile([P, QB, P], F32, name=f"y_sb{v}") for v in range(VB)]
+
+        lanes = keep.tile([P, 4, P], BF16, name="lanes")
 
         def add_bias(b):
             for h in range(2):
@@ -177,18 +180,20 @@ def tile_attend_x_alibi_sink_srt_kernel(tc, qT, kT, vT, vs, pos, slope, sink, of
             nc.scalar.activation(p[b][:, 0 : N + 1], s[b][:, 0 : N + 1], ACT.Exp, bias=neg_max[b][:], accum_out=total[:, b : b + 1])
 
         def turn_weights(b):
-            ps = psum.tile([P, 4, P], F32, tag=f"p{b}", name=f"p_ps{b}")
-            for t in range(4):
-                nc.tensor.transpose(ps[:, t, :], p[b][:, t * P : (t + 1) * P], ident[:])
             if b == 0:
-                lanes = keep.tile([P, 4, P], BF16, name="lanes")
+                pair = [psum.tile([P, 2, P], F32, tag=f"p{u}", name=f"p0_ps{u}") for u in range(2)]
                 for t in range(4):
-                    nc.scalar.activation(lanes[:, t, :], ps[:, t, :], ACT.Copy, scale=vsT[:, t : t + 1])
+                    nc.tensor.transpose(pair[t // 2][:, t % 2, :], p[b][:, t * P : (t + 1) * P], ident[:])
+                for t in range(4):
+                    nc.scalar.activation(lanes[:, t, :], pair[t // 2][:, t % 2, :], ACT.Copy, scale=vsT[:, t : t + 1])
                 nc.scalar.copy(
                     w_in[b][:].rearrange("m (c i) t -> m c t i", i=4),
                     lanes[:].rearrange("m t (c i) -> m c t i", i=4),
                 )
                 return
+            ps = psum.tile([P, 4, P], F32, tag="p2", name="p1_ps")
+            for t in range(4):
+                nc.tensor.transpose(ps[:, t, :], p[b][:, t * P : (t + 1) * P], ident[:])
             nc.vector.tensor_tensor(
                 w_in[b][:],
                 ps[:].rearrange("m t q -> m q t"),
@@ -229,8 +234,6 @@ def tile_attend_x_alibi_sink_srt_kernel(tc, qT, kT, vT, vs, pos, slope, sink, of
         add_bias(1)
         softmax(0)
         softmax(1)
-        for u in range(2):
-            nc.scalar.copy(vsT[:, 2 * u : 2 * u + 2], vsT_ps[u][:, :, P - 1])
         gather_values(0)
         gather_values(1)
         turn_weights(0)
@@ -238,11 +241,11 @@ def tile_attend_x_alibi_sink_srt_kernel(tc, qT, kT, vT, vs, pos, slope, sink, of
         turn_values(0)
         turn_values(1)
         nc.vector.reciprocal(inv[:], total[:])
-        quantise_weights(1)
         quantise_weights(0)
         quantise_values(0)
-        product(1, 0)
+        quantise_weights(1)
         product(0, 0)
+        product(1, 0)
         quantise_values(1)
         product(0, 1)
         product(1, 1)

@@ -228,7 +228,10 @@ def tile_attend_x_alibi_sink_srt_kernel(tc, qT, kT, vT, vs, pos, slope, sink, of
                     nc.scalar.activation(y_sb[v][:, b, :], y[b][v][:], ACT.Copy, scale=inv[:, b : b + 1])
                 else:
                     nc.vector.tensor_scalar(y_sb[v][:, b, :], y[b][v][:], inv[:, b : b + 1], None, ALU.mult)
-            nc.sync.dma_start(out.rearrange("o (b q) e -> q (o b) e", q=P)[:, :, v * P : (v + 1) * P], y_sb[v][:])
+                if v == VB - 1:
+                    nc.sync.dma_start(out[0, b * P : (b + 1) * P, v * P : (v + 1) * P], y_sb[v][:, b, :])
+            if v < VB - 1:
+                nc.sync.dma_start(out.rearrange("o (b q) e -> q (o b) e", q=P)[:, :, v * P : (v + 1) * P], y_sb[v][:])
 
         add_bias(0)
         add_bias(1)

@@ -143,13 +143,13 @@ def tile_attend_x_alibi_sink_srt_kernel(tc, qT, kT, vT, vs, pos, slope, sink, of
         v_scales = keep.tile([P, DV], U8, align_bytes=64, name="v_scales")
 
         def gather_values(b):
-            nc.vector.tensor_copy(v_bf[b], v_raw[b][:].indirect(offsets[:]))
+            nc.vector.tensor_copy(v_bf[b].rearrange("e (u m j) -> e m u j", u=2, j=2), v_raw[b][:].indirect(offsets[:]))
 
         def turn_values(b):
             ps = psum.tile([P, 2, P], F32, tag=f"p{b}", name=f"v_ps{b}")
             words = v_bf[b].bitcast(F32)
             for u in range(2):
-                nc.tensor.transpose(ps[:, u, :], words[:, u::2], ident[:])
+                nc.tensor.transpose(ps[:, u, :], words[:, u * P : (u + 1) * P], ident[:])
             nc.scalar.copy(v_in[b][:].bitcast(F32).rearrange("m (e u) -> m e u", u=2), ps[:].rearrange("m u e -> m e u"))
 
         neg_max = [keep.tile([P, 1], F32, name=f"neg_max{b}") for b in range(QB)]

@@ -68,11 +68,9 @@ def tile_attend_x_alibi_sink_srt_kernel(tc, qT, kT, vT, vs, pos, slope, sink, of
         ident = keep.tile([P, P], F32, name="ident")
         make_identity(nc, ident[:])
 
-        k_bf = keep.tile([P, N, 4], BF16, align_bytes=64, name="k_bf")
         k_pair = late.tile([P, 2, N], BF16, offset=23 * KIB, name="k_pair")
         for t in (0, 1):
             nc.vector.tensor_copy(k_pair[:, t, :], k_raw[t][:].indirect(offsets[:]))
-        nc.scalar.copy(k_bf[:, :, 0:2], k_pair[:].rearrange("p t n -> p n t"))
 
         s = [late.tile([P, N + 4], F32, align_bytes=64, offset=4 * KIB * b, name=f"s{b}") for b in range(QB)]
         cols_ps = psum.tile([P, P], F32, tag="s00", name="cols_ps")
@@ -85,7 +83,7 @@ def tile_attend_x_alibi_sink_srt_kernel(tc, qT, kT, vT, vs, pos, slope, sink, of
         posT_ps = psum.tile([P, 4, P], F32, tag="p0", name="posT_ps")
         for t in range(4):
             nc.tensor.transpose(posT_ps[:, t, :], pos_g[:, t::4], ident[:])
-        posT = keep.tile([P, 4], F32, name="posT")
+        posT = keep.tile([P, 4], F32, align_bytes=64, tag="posT", name="posT")
         nc.scalar.copy(posT[:], posT_ps[:, :, P - 1])
         posb_ps = psum.tile([P, 4, P], F32, tag="p1", name="posb_ps")
         for t in range(4):
@@ -98,6 +96,8 @@ def tile_attend_x_alibi_sink_srt_kernel(tc, qT, kT, vT, vs, pos, slope, sink, of
             nc.tensor.transpose(vsT_ps[:, t, :], vs_g[:, t::4], ident[:])
         vsT = keep.tile([P, 4], F32, name="vsT")
         nc.scalar.copy(vsT[:], vsT_ps[:, :, P - 1])
+        k_bf = keep.tile([P, N, 4], BF16, align_bytes=64, tag="posT", name="k_bf")
+        nc.scalar.copy(k_bf[:, :, 0:2], k_pair[:].rearrange("p t n -> p n t"))
 
         q_in = [keep.tile([P, P, 4], BF16, align_bytes=64, name=f"q_in{b}") for b in range(QB)]
         q_codes = [keep.tile([P, P], U32, align_bytes=64, name=f"q_codes{b}") for b in range(QB)]

@@ -31,17 +31,17 @@ def tile_attend_x_alibi_sink_srt_kernel(tc, qT, kT, vT, vs, pos, slope, sink, of
 
         offsets = keep.tile([P, N // 16], U16, name="offsets")
         k_raw = [keep.tile([P, T], F32, name=f"k_raw{t}") for t in range(4)]
-        q_raw = keep.tile([P, 4, NQ], F32, name="q_raw")
+        q_raw = late.tile([P, 4, NQ], F32, offset=2 * KIB, name="q_raw")
         v_raw = [keep.tile([P, T], F32, name="v_raw0"), late.tile([P, T], F32, offset=8 * KIB, name="v_raw1")]
         rows = keep.tile([P, P], F32, align_bytes=64, tag="rows", name="rows")
         pos_raw = late.tile([P, T], F32, offset=16 * KIB, name="pos_raw")
         vs_raw = late.tile([P, T], F32, offset=24 * KIB, name="vs_raw")
         k_planes = kT.rearrange("(p t) n -> p t n", t=4)
+        nc.sync.dma_start(k_raw[0][:], k_planes[:, 0, :])
         nc.sync.dma_start(offsets[:], offs)
         nc.scalar.dma_start(pos_raw[P - 1 : P, :], pos[0:1, :])
         nc.scalar.dma_start(vs_raw[P - 1 : P, :], vs[0:1, :])
-        for t in (0, 1):
-            nc.sync.dma_start(k_raw[t][:], k_planes[:, t, :])
+        nc.sync.dma_start(k_raw[1][:], k_planes[:, 1, :])
 
         warm = keep.tile([P, 1], F32, name="warm")
         nc.vector.memset(warm[:], 0.0)
@@ -73,12 +73,6 @@ def tile_attend_x_alibi_sink_srt_kernel(tc, qT, kT, vT, vs, pos, slope, sink, of
             nc.vector.tensor_copy(k_pair[:, t, :], k_raw[t][:].indirect(offsets[:]))
 
         s = [late.tile([P, N + 4], F32, align_bytes=64, offset=4 * KIB * b, name=f"s{b}") for b in range(QB)]
-        cols_ps = psum.tile([P, P], F32, tag="s00", name="cols_ps")
-        nc.tensor.transpose(cols_ps[:], rows[:], ident[:])
-        slope_col = keep.tile([P, QB], F32, name="slope_col")
-        nc.scalar.copy(slope_col[:], cols_ps[:, R0 : R0 + QB])
-        for b in range(QB):
-            nc.scalar.copy(s[b][:, N : N + 1], cols_ps[:, R0 + QB + b : R0 + QB + b + 1])
 
         posT_ps = psum.tile([P, 4, P], F32, tag="p0", name="posT_ps")
         for t in range(4):
@@ -96,28 +90,42 @@ def tile_attend_x_alibi_sink_srt_kernel(tc, qT, kT, vT, vs, pos, slope, sink, of
             nc.tensor.transpose(vsT_ps[:, t, :], vs_g[:, t::4], ident[:])
         vsT = keep.tile([P, 4], F32, name="vsT")
         nc.scalar.copy(vsT[:], vsT_ps[:, :, P - 1])
-        k_bf = keep.tile([P, N, 4], BF16, align_bytes=64, tag="posT", name="k_bf")
-        nc.scalar.copy(k_bf[:, :, 0:2], k_pair[:].rearrange("p t n -> p n t"))
+        k_all = keep.tile([P, 4 * N + 4 * H], BF16, align_bytes=64, tag="posT", name="k_all")
+        k_bf = k_all[:, 0 : 4 * N].rearrange("p (n t) -> p n t", t=4)
+        k_head = k_all[:, 4 * N : 4 * N + 4 * H].rearrange("p (u n j) -> p u n j", u=2, j=2)
+        nc.scalar.copy(k_bf[:, H:N, 0:2], k_pair[:, :, H:N].rearrange("p t n -> p n t"))
+        nc.scalar.copy(k_head[:, 0], k_pair[:, :, 0:H].rearrange("p t n -> p n t"))
 
         q_in = [keep.tile([P, P, 4], BF16, align_bytes=64, name=f"q_in{b}") for b in range(QB)]
         q_codes = [keep.tile([P, P], U32, align_bytes=64, name=f"q_codes{b}") for b in range(QB)]
         q_scales = [keep.tile([P, P], U8, align_bytes=64, name=f"q_scales{b}") for b in range(QB)]
         k_codes = keep.tile([P, N], U32, align_bytes=64, name="k_codes")
         k_scales = keep.tile([P, N], U8, align_bytes=64, tag="rows", name="k_scales")
-        nc.vector.tensor_copy(k_bf[:, :, 2], k_raw[2][:].indirect(offsets[:]))
-        nc.vector.tensor_copy(k_bf[:, 0:H, 3], k_raw[3][:, 0:PRE].indirect(offsets[:, 0 : H // 16]))
+        nc.vector.tensor_copy(k_head[:, 1, :, 0], k_raw[2][:].indirect(offsets[:, 0 : H // 16]))
+        nc.vector.tensor_copy(k_bf[:, H:N, 2], k_raw[2][:].indirect(offsets[:, H // 16 : N // 16]))
+        nc.vector.tensor_copy(k_head[:, 1, :, 1], k_raw[3][:, 0:PRE].indirect(offsets[:, 0 : H // 16]))
+        nc.scalar.copy(
+            k_all[:, 0 : 4 * H].bitcast(F32).rearrange("p (n u) -> p n u", u=2),
+            k_all[:, 4 * N : 4 * N + 4 * H].bitcast(F32).rearrange("p (u n) -> p n u", u=2),
+        )
         nc.vector.tensor_copy(k_bf[:, H:N, 3], k_raw[3][:].indirect(offsets[:, H // 16 : N // 16]))
         for b in range(QB):
             nc.scalar.copy(
                 q_in[b][:].rearrange("p (c i) t -> p c t i", i=4),
                 q_raw[:, :, b * P : (b + 1) * P].rearrange("p t (c i) -> p c t i", i=4),
             )
+        slope_ps = psum.tile([P, P], F32, tag="p3", name="slope_ps")
+        nc.tensor.transpose(slope_ps[:], rows[:], ident[:])
+        sink_ps = psum.tile([P, P], F32, tag="p2", name="sink_ps")
+        nc.tensor.transpose(sink_ps[:], rows[:], ident[:])
+        for b in range(QB):
+            nc.scalar.copy(s[b][:, N : N + 1], sink_ps[:, R0 + QB + b : R0 + QB + b + 1])
         for h in range(2):
             ks = slice(h * H, (h + 1) * H)
             nc.vector.quantize_mx(
                 out=k_codes[:, ks].bitcast(FP8X4),
                 scales=k_scales[:, ks],
-                in_=k_bf[:, ks, :].rearrange("p n t -> p (n t)"),
+                in_=k_all[:, 4 * h * H : 4 * (h + 1) * H],
             )
         for b in range(QB):
             nc.vector.quantize_mx(out=q_codes[b][:].bitcast(FP8X4), scales=q_scales[b][:], in_=q_in[b][:].rearrange("p n t -> p (n t)"))
@@ -169,7 +177,7 @@ def tile_attend_x_alibi_sink_srt_kernel(tc, qT, kT, vT, vs, pos, slope, sink, of
                 nc.vector.scalar_tensor_tensor(
                     s[b][:, 0:N].rearrange("q (t m) -> q t m", t=4)[:, :, ms],
                     posb[:, :, ms],
-                    slope_col[:, b : b + 1],
+                    slope_ps[:, R0 + b : R0 + b + 1],
                     scores[b][h][:].rearrange("q (m t) -> q t m", t=4),
                     ALU.mult,
                     ALU.add,

@@ -16,6 +16,8 @@ P = 128
 D, NQ, N, T, DV = 512, 256, 512, 2048, 256
 QB = NQ // P
 VB = DV // P
+H = N // 2
+PRE = T - H
 R0 = P - 4
 KIB = 1024
 FLOPS = 2 * NQ * N * (D + DV)
@@ -30,32 +32,19 @@ def tile_attend_x_alibi_sink_srt_kernel(tc, qT, kT, vT, vs, pos, slope, sink, of
         psum = ctx.enter_context(tc.psum_pool(name="psum", bufs=1))
 
         offsets = keep.tile([P, N // 16], U16, name="offsets")
+        first, second = offsets[:, 0 : H // 16], offsets[:, H // 16 : N // 16]
         k_raw = [keep.tile([P, T], F32, name=f"k_raw{t}") for t in range(4)]
         q_raw = late.tile([P, 4, NQ], F32, offset=2 * KIB, name="q_raw")
-        v_raw = [keep.tile([P, T], F32, name="v_raw0"), late.tile([P, T], F32, offset=8 * KIB, name="v_raw1")]
+        v_raw = [late.tile([P, T], F32, offset=(8 + 8 * b) * KIB, name=f"v_raw{b}") for b in range(VB)]
         rows = keep.tile([P, P], F32, align_bytes=64, tag="rows", name="rows")
-        pos_raw = late.tile([P, T], F32, offset=16 * KIB, name="pos_raw")
-        vs_raw = late.tile([P, T], F32, offset=24 * KIB, name="vs_raw")
+        pos_raw = keep.tile([P, T], F32, name="pos_raw")
+        vs_raw = keep.tile([P, T], F32, name="vs_raw")
         k_planes = kT.rearrange("(p t) n -> p t n", t=4)
         nc.sync.dma_start(k_raw[0][:], k_planes[:, 0, :])
         nc.sync.dma_start(offsets[:], offs)
         nc.scalar.dma_start(pos_raw[P - 1 : P, :], pos[0:1, :])
         nc.scalar.dma_start(vs_raw[P - 1 : P, :], vs[0:1, :])
         nc.sync.dma_start(k_raw[1][:], k_planes[:, 1, :])
-
-        warm = keep.tile([P, 1], F32, name="warm")
-        nc.vector.memset(warm[:], 0.0)
-        nc.scalar.activation(warm[:], warm[:], ACT.Exp)
-
-        nc.vector.memset(pos_raw[0 : P - 1, :], 0.0)
-        nc.vector.memset(vs_raw[0 : P - 1, :], 0.0)
-        nc.vector.memset(rows[0:R0, :], 0.0)
-        pos_g = keep.tile([P, N], F32, name="pos_g")
-        nc.vector.tensor_copy(pos_g[:], pos_raw[:].indirect(offsets[:]))
-        vs_g = keep.tile([P, N], F32, name="vs_g")
-        nc.vector.tensor_copy(vs_g[:], vs_raw[:].indirect(offsets[:]))
-        H = N // 2
-        PRE = T - H
         nc.sync.dma_start(k_raw[2][:], k_planes[:, 2, :])
         nc.sync.dma_start(k_raw[3][:, 0:PRE], k_planes[:, 3, 0:PRE])
         nc.sync.dma_start(k_raw[3][:, PRE:T], k_planes[:, 3, PRE:T])
@@ -65,68 +54,68 @@ def tile_attend_x_alibi_sink_srt_kernel(tc, qT, kT, vT, vs, pos, slope, sink, of
         for b in range(VB):
             nc.sync.dma_start(v_raw[b][:], vT[b * P : (b + 1) * P, :])
 
+        warm = keep.tile([P, 1], F32, name="warm")
+        nc.vector.memset(warm[:], 0.0)
+        nc.scalar.activation(warm[:], warm[:], ACT.Exp)
+
+        nc.vector.memset(pos_raw[0 : P - 1, :], 0.0)
+        nc.vector.memset(rows[0:R0, :], 0.0)
         ident = keep.tile([P, P], F32, name="ident")
         make_identity(nc, ident[:])
+        nc.gpsimd.memset(vs_raw[0 : P - 1, :], 0.0)
 
-        k_pair = late.tile([P, 2, N], BF16, offset=23 * KIB, name="k_pair")
-        for t in (0, 1):
-            nc.vector.tensor_copy(k_pair[:, t, :], k_raw[t][:].indirect(offsets[:]))
-
-        s = [late.tile([P, N + 4], F32, align_bytes=64, offset=4 * KIB * b, name=f"s{b}") for b in range(QB)]
-
+        pos_g = keep.tile([P, N], F32, name="pos_g")
+        nc.scalar.activation(pos_g[:], pos_raw[:].indirect(offsets[:]), ACT.Copy)
+        vs_g = keep.tile([P, N], F32, name="vs_g")
+        nc.scalar.activation(vs_g[:], vs_raw[:].indirect(offsets[:]), ACT.Copy)
         posT_ps = psum.tile([P, 4, P], F32, tag="p0", name="posT_ps")
         for t in range(4):
             nc.tensor.transpose(posT_ps[:, t, :], pos_g[:, t::4], ident[:])
-        posT = keep.tile([P, 4], F32, align_bytes=64, tag="posT", name="posT")
+        posT = keep.tile([P, 4], F32, name="posT")
         nc.scalar.copy(posT[:], posT_ps[:, :, P - 1])
         posb_ps = psum.tile([P, 4, P], F32, tag="p1", name="posb_ps")
         for t in range(4):
             nc.tensor.transpose(posb_ps[:, t, :], posT[:, t : t + 1].to_broadcast([P, P]), ident[:])
-        posb = keep.tile([P, 4, P], F32, tag="posb", name="posb")
+        posb = keep.tile([P, 4, P], F32, align_bytes=64, tag="posb", name="posb")
         nc.scalar.copy(posb[:], posb_ps[:])
-
         vsT_ps = psum.tile([P, 4, P], F32, tag="p2", name="vsT_ps")
         for t in range(4):
             nc.tensor.transpose(vsT_ps[:, t, :], vs_g[:, t::4], ident[:])
         vsT = keep.tile([P, 4], F32, name="vsT")
         nc.scalar.copy(vsT[:], vsT_ps[:, :, P - 1])
-        k_all = keep.tile([P, 4 * N + 4 * H], BF16, align_bytes=64, tag="posT", name="k_all")
-        k_bf = k_all[:, 0 : 4 * N].rearrange("p (n t) -> p n t", t=4)
-        k_head = k_all[:, 4 * N : 4 * N + 4 * H].rearrange("p (u n j) -> p u n j", u=2, j=2)
-        nc.scalar.copy(k_bf[:, H:N, 0:2], k_pair[:, :, H:N].rearrange("p t n -> p n t"))
-        nc.scalar.copy(k_head[:, 0], k_pair[:, :, 0:H].rearrange("p t n -> p n t"))
+
+        k_in = [keep.tile([P, H, 4], BF16, align_bytes=64, name=f"k_in{h}") for h in range(2)]
+        k_pairs = keep.tile([P, 2, H, 2], BF16, name="k_pairs")
+        for t in range(4):
+            window = k_raw[t][:, 0:PRE] if t == 3 else k_raw[t][:]
+            nc.vector.tensor_copy(k_pairs[:, t // 2, :, t % 2], window.indirect(first))
+            nc.vector.tensor_copy(k_in[1][:, :, t], k_raw[t][:].indirect(second))
+        nc.scalar.copy(
+            k_in[0][:].rearrange("p n t -> p (n t)").bitcast(F32).rearrange("p (n u) -> p n u", u=2),
+            k_pairs[:].rearrange("p u n j -> p (u n j)").bitcast(F32).rearrange("p (u n) -> p n u", u=2),
+        )
 
         q_in = [keep.tile([P, P, 4], BF16, align_bytes=64, name=f"q_in{b}") for b in range(QB)]
-        q_codes = [keep.tile([P, P], U32, align_bytes=64, name=f"q_codes{b}") for b in range(QB)]
-        q_scales = [keep.tile([P, P], U8, align_bytes=64, name=f"q_scales{b}") for b in range(QB)]
-        k_codes = keep.tile([P, N], U32, align_bytes=64, name="k_codes")
-        k_scales = keep.tile([P, N], U8, align_bytes=64, tag="rows", name="k_scales")
-        nc.vector.tensor_copy(k_head[:, 1, :, 0], k_raw[2][:].indirect(offsets[:, 0 : H // 16]))
-        nc.vector.tensor_copy(k_bf[:, H:N, 2], k_raw[2][:].indirect(offsets[:, H // 16 : N // 16]))
-        nc.vector.tensor_copy(k_head[:, 1, :, 1], k_raw[3][:, 0:PRE].indirect(offsets[:, 0 : H // 16]))
-        nc.scalar.copy(
-            k_all[:, 0 : 4 * H].bitcast(F32).rearrange("p (n u) -> p n u", u=2),
-            k_all[:, 4 * N : 4 * N + 4 * H].bitcast(F32).rearrange("p (u n) -> p n u", u=2),
-        )
-        nc.vector.tensor_copy(k_bf[:, H:N, 3], k_raw[3][:].indirect(offsets[:, H // 16 : N // 16]))
         for b in range(QB):
             nc.scalar.copy(
                 q_in[b][:].rearrange("p (c i) t -> p c t i", i=4),
                 q_raw[:, :, b * P : (b + 1) * P].rearrange("p t (c i) -> p c t i", i=4),
             )
+        s = [late.tile([P, N + 4], F32, align_bytes=64, offset=4 * KIB * b, name=f"s{b}") for b in range(QB)]
         slope_ps = psum.tile([P, P], F32, tag="p3", name="slope_ps")
         nc.tensor.transpose(slope_ps[:], rows[:], ident[:])
         sink_ps = psum.tile([P, P], F32, tag="p2", name="sink_ps")
         nc.tensor.transpose(sink_ps[:], rows[:], ident[:])
         for b in range(QB):
             nc.scalar.copy(s[b][:, N : N + 1], sink_ps[:, R0 + QB + b : R0 + QB + b + 1])
+
+        k_codes = keep.tile([P, N], U32, align_bytes=64, name="k_codes")
+        k_scales = keep.tile([P, N], U8, align_bytes=64, tag="rows", name="k_scales")
         for h in range(2):
             ks = slice(h * H, (h + 1) * H)
-            nc.vector.quantize_mx(
-                out=k_codes[:, ks].bitcast(FP8X4),
-                scales=k_scales[:, ks],
-                in_=k_all[:, 4 * h * H : 4 * (h + 1) * H],
-            )
+            nc.vector.quantize_mx(out=k_codes[:, ks].bitcast(FP8X4), scales=k_scales[:, ks], in_=k_in[h][:].rearrange("p n t -> p (n t)"))
+        q_codes = [keep.tile([P, P], U32, align_bytes=64, name=f"q_codes{b}") for b in range(QB)]
+        q_scales = [keep.tile([P, P], U8, align_bytes=64, name=f"q_scales{b}") for b in range(QB)]
         for b in range(QB):
             nc.vector.quantize_mx(out=q_codes[b][:].bitcast(FP8X4), scales=q_scales[b][:], in_=q_in[b][:].rearrange("p n t -> p (n t)"))
 
@@ -144,32 +133,18 @@ def tile_attend_x_alibi_sink_srt_kernel(tc, qT, kT, vT, vs, pos, slope, sink, of
                     stop=True,
                 )
 
-        v_all = keep.tile([P, VB * N], BF16, tag="posb", name="v_all")
-        v_bf = [v_all[:, b * N : (b + 1) * N] for b in range(VB)]
-        v_in = [keep.tile([P, 4 * P], BF16, align_bytes=64, name=f"v_in{b}") for b in range(VB)]
-        v_codes = late.tile([P, DV], U32, align_bytes=64, offset=8 * KIB, name="v_codes")
-        v_scales = keep.tile([P, DV], U8, align_bytes=64, name="v_scales")
-
-        def gather_values(b):
-            nc.vector.tensor_copy(v_bf[b].rearrange("e (u m j) -> e m u j", u=2, j=2), v_raw[b][:].indirect(offsets[:]))
-
-        def turn_values(b):
-            ps = psum.tile([P, 2, P], F32, tag=f"p{b}", name=f"v_ps{b}")
-            words = v_bf[b].bitcast(F32)
-            for u in range(2):
-                nc.tensor.transpose(ps[:, u, :], words[:, u * P : (u + 1) * P], ident[:])
-            nc.scalar.copy(v_in[b][:].bitcast(F32).rearrange("m (e u) -> m e u", u=2), ps[:].rearrange("m u e -> m e u"))
-
         neg_max = [keep.tile([P, 1], F32, name=f"neg_max{b}") for b in range(QB)]
         total = keep.tile([P, QB], F32, name="total")
         inv = keep.tile([P, QB], F32, name="inv")
-        p = [keep.tile([P, N + 4], F32, name=f"p{b}") for b in range(QB)]
-        w_in = [keep.tile([P, P, 4], BF16, align_bytes=64, name="w_in0"), keep.tile([P, P, 4], BF16, align_bytes=64, name="w_in1")]
+        p = [late.tile([P, N + 4], F32, offset=8 * KIB, name="p0"), keep.tile([P, N + 4], F32, name="p1")]
+        v_bf = [keep.tile([P, N], BF16, name="v_bf0"), late.tile([P, N], BF16, offset=4 * KIB, name="v_bf1")]
+        v_in = [keep.tile([P, 4 * P], BF16, align_bytes=64, tag="posb", name="v_in0"), keep.tile([P, 4 * P], BF16, align_bytes=64, name="v_in1")]
+        v_codes = [keep.tile([P, P], U32, align_bytes=64, name=f"v_codes{v}") for v in range(VB)]
+        v_scales = [keep.tile([P, P], U8, align_bytes=64, name=f"v_scales{v}") for v in range(VB)]
+        w_in = [keep.tile([P, P, 4], BF16, align_bytes=64, name=f"w_in{b}") for b in range(QB)]
         w_codes = [keep.tile([P, P], U32, align_bytes=64, name=f"w_codes{b}") for b in range(QB)]
         w_scales = [keep.tile([P, P], U8, align_bytes=64, name=f"w_scales{b}") for b in range(QB)]
         y_sb = [keep.tile([P, QB, P], F32, name=f"y_sb{v}") for v in range(VB)]
-
-        lanes = keep.tile([P, 4, P], BF16, name="lanes")
 
         def add_bias(b):
             for h in range(2):
@@ -187,19 +162,18 @@ def tile_attend_x_alibi_sink_srt_kernel(tc, qT, kT, vT, vs, pos, slope, sink, of
             nc.vector.tensor_reduce(neg_max[b][:], s[b][:, 0 : N + 1], mybir.AxisListType.X, ALU.max, negate=True)
             nc.scalar.activation(p[b][:, 0 : N + 1], s[b][:, 0 : N + 1], ACT.Exp, bias=neg_max[b][:], accum_out=total[:, b : b + 1])
 
+        def gather_values(v):
+            nc.scalar.activation(v_bf[v][:], v_raw[v][:].indirect(offsets[:]), ACT.Copy)
+
+        def turn_values(v, copy):
+            ps = psum.tile([P, 2, P], F32, tag=f"p{3 * v}", name=f"v_ps{v}")
+            words = v_bf[v][:].bitcast(F32)
+            for u in range(2):
+                nc.tensor.transpose(ps[:, u, :], words[:, u::2], ident[:])
+            copy(v_in[v][:].bitcast(F32).rearrange("m (e u) -> m e u", u=2), ps[:].rearrange("m u e -> m e u"))
+
         def turn_weights(b):
-            if b == 0:
-                pair = [psum.tile([P, 2, P], F32, tag=f"p{u}", name=f"p0_ps{u}") for u in range(2)]
-                for t in range(4):
-                    nc.tensor.transpose(pair[t // 2][:, t % 2, :], p[b][:, t * P : (t + 1) * P], ident[:])
-                for t in range(4):
-                    nc.scalar.activation(lanes[:, t, :], pair[t // 2][:, t % 2, :], ACT.Copy, scale=vsT[:, t : t + 1])
-                nc.scalar.copy(
-                    w_in[b][:].rearrange("m (c i) t -> m c t i", i=4),
-                    lanes[:].rearrange("m t (c i) -> m c t i", i=4),
-                )
-                return
-            ps = psum.tile([P, 4, P], F32, tag="p2", name="p1_ps")
+            ps = psum.tile([P, 4, P], F32, tag=f"p{1 + b}", name=f"p_ps{b}")
             for t in range(4):
                 nc.tensor.transpose(ps[:, t, :], p[b][:, t * P : (t + 1) * P], ident[:])
             nc.vector.tensor_tensor(
@@ -212,20 +186,18 @@ def tile_attend_x_alibi_sink_srt_kernel(tc, qT, kT, vT, vs, pos, slope, sink, of
         def quantise_weights(b):
             nc.vector.quantize_mx(out=w_codes[b][:].bitcast(FP8X4), scales=w_scales[b][:], in_=w_in[b][:].rearrange("m q t -> m (q t)"))
 
-        def quantise_values(b):
-            es = slice(b * P, (b + 1) * P)
-            nc.vector.quantize_mx(out=v_codes[:, es].bitcast(FP8X4), scales=v_scales[:, es], in_=v_in[b][:])
+        def quantise_values(v):
+            nc.vector.quantize_mx(out=v_codes[v][:].bitcast(FP8X4), scales=v_scales[v][:], in_=v_in[v][:])
 
         y = [[psum.tile([P, P], F32, tag=f"s{b}{v}", name=f"y{b}{v}") for v in range(VB)] for b in range(QB)]
 
         def product(b, v):
-            es = slice(v * P, (v + 1) * P)
             nc.tensor.matmul_mx(
                 out=y[b][v][:],
                 lhsT=w_codes[b][:].bitcast(FP8X4),
                 lhsT_scale=w_scales[b][:],
-                rhs=v_codes[:, es].bitcast(FP8X4),
-                rhs_scale=v_scales[:, es],
+                rhs=v_codes[v][:].bitcast(FP8X4),
+                rhs_scale=v_scales[v][:],
                 start=True,
                 stop=True,
             )
@@ -241,19 +213,19 @@ def tile_attend_x_alibi_sink_srt_kernel(tc, qT, kT, vT, vs, pos, slope, sink, of
             if v < VB - 1:
                 nc.sync.dma_start(out.rearrange("o (b q) e -> q (o b) e", q=P)[:, :, v * P : (v + 1) * P], y_sb[v][:])
 
+        gather_values(0)
         add_bias(0)
         add_bias(1)
         softmax(0)
         softmax(1)
-        gather_values(0)
+        turn_values(0, nc.vector.tensor_copy)
         gather_values(1)
         turn_weights(0)
         turn_weights(1)
-        turn_values(0)
-        turn_values(1)
+        turn_values(1, nc.scalar.copy)
+        quantise_values(0)
         nc.vector.reciprocal(inv[:], total[:])
         quantise_weights(0)
-        quantise_values(0)
         quantise_weights(1)
         product(0, 0)
         product(1, 0)

@@ -19,6 +19,7 @@ VB = DV // P
 H = N // 2
 PRE = T - H
 R0 = P - 4
+SHARE = 256
 KIB = 1024
 FLOPS = 2 * NQ * N * (D + DV)
 BYTES = 4 * (D * NQ + D * T + DV * T + 2 * T + 2 * NQ + NQ * DV) + 2 * P * (N // 16)
@@ -42,8 +43,8 @@ def tile_attend_x_alibi_sink_srt_kernel(tc, qT, kT, vT, vs, pos, slope, sink, of
         k_planes = kT.rearrange("(p t) n -> p t n", t=4)
         nc.sync.dma_start(k_raw[0][:], k_planes[:, 0, :])
         nc.sync.dma_start(offsets[:], offs)
-        nc.scalar.dma_start(pos_raw[P - 1 : P, :], pos[0:1, :])
         nc.scalar.dma_start(vs_raw[P - 1 : P, :], vs[0:1, :])
+        nc.scalar.dma_start(pos_raw[P - 1 : P, :], pos[0:1, :])
         nc.sync.dma_start(k_raw[1][:], k_planes[:, 1, :])
         nc.sync.dma_start(k_raw[2][:], k_planes[:, 2, :])
         nc.sync.dma_start(k_raw[3][:, 0:PRE], k_planes[:, 3, 0:PRE])
@@ -58,33 +59,40 @@ def tile_attend_x_alibi_sink_srt_kernel(tc, qT, kT, vT, vs, pos, slope, sink, of
         nc.vector.memset(warm[:], 0.0)
         nc.scalar.activation(warm[:], warm[:], ACT.Exp)
 
-        nc.vector.memset(pos_raw[0 : P - 1, :], 0.0)
+        nc.vector.memset(vs_raw[0 : P - 1, :], 0.0)
         nc.vector.memset(rows[0:R0, :], 0.0)
         ident = keep.tile([P, P], F32, name="ident")
         make_identity(nc, ident[:])
-        nc.gpsimd.memset(vs_raw[0 : P - 1, :], 0.0)
+        nc.gpsimd.memset(pos_raw[0 : P - 1, :], 0.0)
 
-        pos_g = keep.tile([P, N], F32, name="pos_g")
-        nc.scalar.activation(pos_g[:], pos_raw[:].indirect(offsets[:]), ACT.Copy)
         vs_g = keep.tile([P, N], F32, name="vs_g")
         nc.scalar.activation(vs_g[:], vs_raw[:].indirect(offsets[:]), ACT.Copy)
+        pos_g = keep.tile([P, N], F32, name="pos_g")
+        nc.scalar.activation(pos_g[:], pos_raw[:].indirect(offsets[:]), ACT.Copy)
+        vsT_ps = psum.tile([P, 4, P], F32, tag="p2", name="vsT_ps")
+        for t in range(4):
+            nc.tensor.transpose(vsT_ps[:, t, :], vs_g[:, t::4], ident[:])
+        vsT = keep.tile([P, 4], F32, name="vsT")
+        nc.scalar.copy(vsT[:], vsT_ps[:, :, P - 1])
+        vsb_ps = psum.tile([P, 4, P], F32, tag="s00", name="vsb_ps")
+        for t in range(4):
+            nc.tensor.transpose(vsb_ps[:, t, :], vsT[:, t : t + 1].to_broadcast([P, P]), ident[:])
+        vsb = keep.tile([P, P, 4], F32, name="vsb")
+        nc.scalar.copy(vsb[:], vsb_ps[:].rearrange("q t m -> q m t"))
         posT_ps = psum.tile([P, 4, P], F32, tag="p0", name="posT_ps")
         for t in range(4):
             nc.tensor.transpose(posT_ps[:, t, :], pos_g[:, t::4], ident[:])
-        posT = keep.tile([P, 4], F32, name="posT")
+        posT = keep.tile([P, 4], F32, align_bytes=64, tag="posT", name="posT")
         nc.scalar.copy(posT[:], posT_ps[:, :, P - 1])
         posb_ps = psum.tile([P, 4, P], F32, tag="p1", name="posb_ps")
         for t in range(4):
             nc.tensor.transpose(posb_ps[:, t, :], posT[:, t : t + 1].to_broadcast([P, P]), ident[:])
         posb = keep.tile([P, 4, P], F32, align_bytes=64, tag="posb", name="posb")
         nc.scalar.copy(posb[:], posb_ps[:])
-        vsT_ps = psum.tile([P, 4, P], F32, tag="p2", name="vsT_ps")
-        for t in range(4):
-            nc.tensor.transpose(vsT_ps[:, t, :], vs_g[:, t::4], ident[:])
-        vsT = keep.tile([P, 4], F32, name="vsT")
-        nc.scalar.copy(vsT[:], vsT_ps[:, :, P - 1])
+        posn = keep.tile([P, P, 4], F32, name="posn")
+        nc.scalar.copy(posn[:], posb_ps[:].rearrange("q t m -> q m t"))
 
-        k_in = [keep.tile([P, H, 4], BF16, align_bytes=64, name=f"k_in{h}") for h in range(2)]
+        k_in = [keep.tile([P, H, 4], BF16, align_bytes=64, tag="posT", name="k_in0"), keep.tile([P, H, 4], BF16, align_bytes=64, name="k_in1")]
         k_pairs = keep.tile([P, 2, H, 2], BF16, name="k_pairs")
         for t in range(4):
             window = k_raw[t][:, 0:PRE] if t == 3 else k_raw[t][:]
@@ -134,14 +142,17 @@ def tile_attend_x_alibi_sink_srt_kernel(tc, qT, kT, vT, vs, pos, slope, sink, of
                 )
 
         neg_max = [keep.tile([P, 1], F32, name=f"neg_max{b}") for b in range(QB)]
-        total = keep.tile([P, QB], F32, name="total")
+        part = keep.tile([P, QB, 2], F32, name="part")
+        nc.vector.memset(part[:, 0, 1:2], 0.0)
+        total = late.tile([P, QB], F32, offset=18 * KIB, name="total")
         inv = keep.tile([P, QB], F32, name="inv")
-        p = [late.tile([P, N + 4], F32, offset=8 * KIB, name="p0"), keep.tile([P, N + 4], F32, name="p1")]
-        v_bf = [keep.tile([P, N], BF16, name="v_bf0"), late.tile([P, N], BF16, offset=4 * KIB, name="v_bf1")]
+        w_pairs = keep.tile([P, 2, P, 2], BF16, name="w_pairs")
+        p = [late.tile([P, N + 4], F32, offset=8 * KIB, name="p0"), late.tile([P, N + 4], F32, offset=24 * KIB, name="p1")]
+        v_bf = [keep.tile([P, N], BF16, name="v_bf0"), keep.tile([P, N], BF16, name="v_bf1")]
         v_in = [keep.tile([P, 4 * P], BF16, align_bytes=64, tag="posb", name="v_in0"), keep.tile([P, 4 * P], BF16, align_bytes=64, name="v_in1")]
-        v_codes = [keep.tile([P, P], U32, align_bytes=64, name=f"v_codes{v}") for v in range(VB)]
+        v_codes = [late.tile([P, P], U32, align_bytes=64, offset=8 * KIB, name="v_codes0"), keep.tile([P, P], U32, align_bytes=64, name="v_codes1")]
         v_scales = [keep.tile([P, P], U8, align_bytes=64, name=f"v_scales{v}") for v in range(VB)]
-        w_in = [keep.tile([P, P, 4], BF16, align_bytes=64, name=f"w_in{b}") for b in range(QB)]
+        w_in = [late.tile([P, P, 4], BF16, align_bytes=64, offset=(16 + b) * KIB, name=f"w_in{b}") for b in range(QB)]
         w_codes = [keep.tile([P, P], U32, align_bytes=64, name=f"w_codes{b}") for b in range(QB)]
         w_scales = [keep.tile([P, P], U8, align_bytes=64, name=f"w_scales{b}") for b in range(QB)]
         y_sb = [keep.tile([P, QB, P], F32, name=f"y_sb{v}") for v in range(VB)]
@@ -149,6 +160,16 @@ def tile_attend_x_alibi_sink_srt_kernel(tc, qT, kT, vT, vs, pos, slope, sink, of
         def add_bias(b):
             for h in range(2):
                 ms = slice(h * P // 2, (h + 1) * P // 2)
+                if b == 0:
+                    nc.vector.scalar_tensor_tensor(
+                        s[b][:, h * H : (h + 1) * H],
+                        posn[:, ms, :].rearrange("q m t -> q (m t)"),
+                        slope_ps[:, R0 + b : R0 + b + 1],
+                        scores[b][h][:],
+                        ALU.mult,
+                        ALU.add,
+                    )
+                    continue
                 nc.vector.scalar_tensor_tensor(
                     s[b][:, 0:N].rearrange("q (t m) -> q t m", t=4)[:, :, ms],
                     posb[:, :, ms],
@@ -160,10 +181,15 @@ def tile_attend_x_alibi_sink_srt_kernel(tc, qT, kT, vT, vs, pos, slope, sink, of
 
         def softmax(b):
             nc.vector.tensor_reduce(neg_max[b][:], s[b][:, 0 : N + 1], mybir.AxisListType.X, ALU.max, negate=True)
-            nc.scalar.activation(p[b][:, 0 : N + 1], s[b][:, 0 : N + 1], ACT.Exp, bias=neg_max[b][:], accum_out=total[:, b : b + 1])
+            pieces = (slice(0, N + 1),) if b == 0 else (slice(0, H), slice(H, N + 1))
+            for u, cols in enumerate(pieces):
+                nc.scalar.activation(p[b][:, cols], s[b][:, cols], ACT.Exp, bias=neg_max[b][:], accum_out=part[:, b, u : u + 1])
 
         def gather_values(v):
-            nc.scalar.activation(v_bf[v][:], v_raw[v][:].indirect(offsets[:]), ACT.Copy)
+            n = SHARE * v
+            if n:
+                nc.vector.tensor_copy(v_bf[v][:, 0:n], v_raw[v][:].indirect(offsets[:, 0 : n // 16]))
+            nc.scalar.activation(v_bf[v][:, n:N], v_raw[v][:].indirect(offsets[:, n // 16 : N // 16]), ACT.Copy)
 
         def turn_values(v, copy):
             ps = psum.tile([P, 2, P], F32, tag=f"p{3 * v}", name=f"v_ps{v}")
@@ -171,6 +197,21 @@ def tile_attend_x_alibi_sink_srt_kernel(tc, qT, kT, vT, vs, pos, slope, sink, of
             for u in range(2):
                 nc.tensor.transpose(ps[:, u, :], words[:, u::2], ident[:])
             copy(v_in[v][:].bitcast(F32).rearrange("m (e u) -> m e u", u=2), ps[:].rearrange("m u e -> m e u"))
+
+        def scale_first_weights():
+            nc.vector.tensor_tensor(
+                w_pairs[:].rearrange("q u m j -> q m u j"),
+                p[0][:, 0:N].rearrange("q (m u j) -> q m u j", u=2, j=2),
+                vsb[:].rearrange("q m (u j) -> q m u j", u=2),
+                ALU.mult,
+            )
+
+        def turn_first_weights():
+            ps = psum.tile([P, 2, P], F32, tag="p1", name="w_ps")
+            words = w_pairs[:].rearrange("q u m j -> q (u m j)").bitcast(F32)
+            for u in range(2):
+                nc.tensor.transpose(ps[:, u, :], words[:, u * P : (u + 1) * P], ident[:])
+            nc.scalar.copy(w_in[0][:].rearrange("m q t -> m (q t)").bitcast(F32).rearrange("m (q u) -> m q u", u=2), ps[:].rearrange("m u q -> m q u"))
 
         def turn_weights(b):
             ps = psum.tile([P, 4, P], F32, tag=f"p{1 + b}", name=f"p_ps{b}")
@@ -219,14 +260,16 @@ def tile_attend_x_alibi_sink_srt_kernel(tc, qT, kT, vT, vs, pos, slope, sink, of
         softmax(0)
         softmax(1)
         turn_values(0, nc.vector.tensor_copy)
+        scale_first_weights()
         gather_values(1)
-        turn_weights(0)
         turn_weights(1)
+        turn_first_weights()
         turn_values(1, nc.scalar.copy)
         quantise_values(0)
-        nc.vector.reciprocal(inv[:], total[:])
         quantise_weights(0)
+        nc.vector.tensor_reduce(total[:], part[:], mybir.AxisListType.X, ALU.add)
         quantise_weights(1)
+        nc.vector.reciprocal(inv[:], total[:])
         product(0, 0)
         product(1, 0)
         quantise_values(1)

@@ -19,7 +19,8 @@ VB = DV // P
 H = N // 2
 PRE = T - H
 R0 = P - 4
-SHARE = 256
+LEAD = 384
+SHARE = 320
 KIB = 1024
 FLOPS = 2 * NQ * N * (D + DV)
 BYTES = 4 * (D * NQ + D * T + DV * T + 2 * T + 2 * NQ + NQ * DV) + 2 * P * (N // 16)
@@ -87,8 +88,9 @@ def tile_attend_x_alibi_sink_srt_kernel(tc, qT, kT, vT, vs, pos, slope, sink, of
         posb_ps = psum.tile([P, 4, P], F32, tag="p1", name="posb_ps")
         for t in range(4):
             nc.tensor.transpose(posb_ps[:, t, :], posT[:, t : t + 1].to_broadcast([P, P]), ident[:])
-        posb = keep.tile([P, 4, P], F32, align_bytes=64, tag="posb", name="posb")
-        nc.scalar.copy(posb[:], posb_ps[:])
+        v0_and_posb = keep.tile([P, LEAD + 2 * N], BF16, name="v0_and_posb")
+        posb = v0_and_posb[:, LEAD : LEAD + 2 * N].bitcast(F32).rearrange("q (t m) -> q t m", t=4)
+        nc.scalar.copy(posb, posb_ps[:])
         posn = keep.tile([P, P, 4], F32, name="posn")
         nc.scalar.copy(posn[:], posb_ps[:].rearrange("q t m -> q m t"))
 
@@ -142,15 +144,13 @@ def tile_attend_x_alibi_sink_srt_kernel(tc, qT, kT, vT, vs, pos, slope, sink, of
                 )
 
         neg_max = [keep.tile([P, 1], F32, name=f"neg_max{b}") for b in range(QB)]
-        part = keep.tile([P, QB, 2], F32, name="part")
-        nc.vector.memset(part[:, 0, 1:2], 0.0)
-        total = late.tile([P, QB], F32, offset=18 * KIB, name="total")
-        inv = keep.tile([P, QB], F32, name="inv")
-        w_pairs = keep.tile([P, 2, P, 2], BF16, name="w_pairs")
-        p = [late.tile([P, N + 4], F32, offset=8 * KIB, name="p0"), late.tile([P, N + 4], F32, offset=24 * KIB, name="p1")]
-        v_bf = [keep.tile([P, N], BF16, name="v_bf0"), keep.tile([P, N], BF16, name="v_bf1")]
-        v_in = [keep.tile([P, 4 * P], BF16, align_bytes=64, tag="posb", name="v_in0"), keep.tile([P, 4 * P], BF16, align_bytes=64, name="v_in1")]
-        v_codes = [late.tile([P, P], U32, align_bytes=64, offset=8 * KIB, name="v_codes0"), keep.tile([P, P], U32, align_bytes=64, name="v_codes1")]
+        total = keep.tile([P, QB], F32, name="total")
+        inv = late.tile([P, QB], F32, offset=20 * KIB, name="inv")
+        w_pairs = keep.tile([P, N], BF16, name="w_pairs")
+        p = [keep.tile([P, N + 4], F32, name=f"p{b}") for b in range(QB)]
+        v_bf = [v0_and_posb[:, 0:N], keep.tile([P, N], BF16, name="v_bf1")[:]]
+        v_in = [late.tile([P, 4 * P], BF16, align_bytes=64, offset=19 * KIB, name="v_in0"), keep.tile([P, 4 * P], BF16, align_bytes=64, name="v_in1")]
+        v_codes = [keep.tile([P, P], U32, align_bytes=64, name=f"v_codes{v}") for v in range(VB)]
         v_scales = [keep.tile([P, P], U8, align_bytes=64, name=f"v_scales{v}") for v in range(VB)]
         w_in = [late.tile([P, P, 4], BF16, align_bytes=64, offset=(16 + b) * KIB, name=f"w_in{b}") for b in range(QB)]
         w_codes = [keep.tile([P, P], U32, align_bytes=64, name=f"w_codes{b}") for b in range(QB)]
@@ -181,36 +181,30 @@ def tile_attend_x_alibi_sink_srt_kernel(tc, qT, kT, vT, vs, pos, slope, sink, of
 
         def softmax(b):
             nc.vector.tensor_reduce(neg_max[b][:], s[b][:, 0 : N + 1], mybir.AxisListType.X, ALU.max, negate=True)
-            pieces = (slice(0, N + 1),) if b == 0 else (slice(0, H), slice(H, N + 1))
-            for u, cols in enumerate(pieces):
-                nc.scalar.activation(p[b][:, cols], s[b][:, cols], ACT.Exp, bias=neg_max[b][:], accum_out=part[:, b, u : u + 1])
+            nc.scalar.activation(p[b][:, 0 : N + 1], s[b][:, 0 : N + 1], ACT.Exp, bias=neg_max[b][:], accum_out=total[:, b : b + 1])
 
-        def gather_values(v):
-            n = SHARE * v
-            if n:
-                nc.vector.tensor_copy(v_bf[v][:, 0:n], v_raw[v][:].indirect(offsets[:, 0 : n // 16]))
-            nc.scalar.activation(v_bf[v][:, n:N], v_raw[v][:].indirect(offsets[:, n // 16 : N // 16]), ACT.Copy)
+        def gather_values(v, lo, hi, on_vector):
+            window = v_raw[v][:].indirect(offsets[:, lo // 16 : hi // 16])
+            if on_vector:
+                nc.vector.tensor_copy(v_bf[v][:, lo:hi], window)
+            else:
+                nc.scalar.activation(v_bf[v][:, lo:hi], window, ACT.Copy)
 
         def turn_values(v, copy):
             ps = psum.tile([P, 2, P], F32, tag=f"p{3 * v}", name=f"v_ps{v}")
-            words = v_bf[v][:].bitcast(F32)
+            words = v_bf[v].bitcast(F32)
             for u in range(2):
                 nc.tensor.transpose(ps[:, u, :], words[:, u::2], ident[:])
             copy(v_in[v][:].bitcast(F32).rearrange("m (e u) -> m e u", u=2), ps[:].rearrange("m u e -> m e u"))
 
         def scale_first_weights():
-            nc.vector.tensor_tensor(
-                w_pairs[:].rearrange("q u m j -> q m u j"),
-                p[0][:, 0:N].rearrange("q (m u j) -> q m u j", u=2, j=2),
-                vsb[:].rearrange("q m (u j) -> q m u j", u=2),
-                ALU.mult,
-            )
+            nc.vector.tensor_tensor(w_pairs[:], p[0][:, 0:N], vsb[:].rearrange("q m t -> q (m t)"), ALU.mult)
 
         def turn_first_weights():
             ps = psum.tile([P, 2, P], F32, tag="p1", name="w_ps")
-            words = w_pairs[:].rearrange("q u m j -> q (u m j)").bitcast(F32)
+            words = w_pairs[:].bitcast(F32)
             for u in range(2):
-                nc.tensor.transpose(ps[:, u, :], words[:, u * P : (u + 1) * P], ident[:])
+                nc.tensor.transpose(ps[:, u, :], words[:, u::2], ident[:])
             nc.scalar.copy(w_in[0][:].rearrange("m q t -> m (q t)").bitcast(F32).rearrange("m (q u) -> m q u", u=2), ps[:].rearrange("m u q -> m q u"))
 
         def turn_weights(b):
@@ -254,22 +248,23 @@ def tile_attend_x_alibi_sink_srt_kernel(tc, qT, kT, vT, vs, pos, slope, sink, of
             if v < VB - 1:
                 nc.sync.dma_start(out.rearrange("o (b q) e -> q (o b) e", q=P)[:, :, v * P : (v + 1) * P], y_sb[v][:])
 
-        gather_values(0)
+        gather_values(0, 0, LEAD, False)
         add_bias(0)
         add_bias(1)
         softmax(0)
         softmax(1)
-        turn_values(0, nc.vector.tensor_copy)
+        gather_values(0, LEAD, N, True)
         scale_first_weights()
-        gather_values(1)
+        gather_values(1, 0, SHARE, True)
+        gather_values(1, SHARE, N, False)
+        turn_values(0, nc.scalar.copy)
         turn_weights(1)
         turn_first_weights()
         turn_values(1, nc.scalar.copy)
         quantise_values(0)
         quantise_weights(0)
-        nc.vector.tensor_reduce(total[:], part[:], mybir.AxisListType.X, ALU.add)
-        quantise_weights(1)
         nc.vector.reciprocal(inv[:], total[:])
+        quantise_weights(1)
         product(0, 0)
         product(1, 0)
         quantise_values(1)

@@ -19,8 +19,8 @@ VB = DV // P
 H = N // 2
 PRE = T - H
 R0 = P - 4
-LEAD = 384
-SHARE = 320
+LEAD = 448
+SHARE = 288
 KIB = 1024
 FLOPS = 2 * NQ * N * (D + DV)
 BYTES = 4 * (D * NQ + D * T + DV * T + 2 * T + 2 * NQ + NQ * DV) + 2 * P * (N // 16)
@@ -145,14 +145,17 @@ def tile_attend_x_alibi_sink_srt_kernel(tc, qT, kT, vT, vs, pos, slope, sink, of
 
         neg_max = [keep.tile([P, 1], F32, name=f"neg_max{b}") for b in range(QB)]
         total = keep.tile([P, QB], F32, name="total")
-        inv = late.tile([P, QB], F32, offset=20 * KIB, name="inv")
-        w_pairs = keep.tile([P, N], BF16, name="w_pairs")
-        p = [keep.tile([P, N + 4], F32, name=f"p{b}") for b in range(QB)]
+        inv = keep.tile([P, QB], F32, name="inv")
+        both = late.tile([P, QB], F32, offset=24 * KIB, name="both")
+        rest = keep.tile([P, QB], F32, name="rest")
+        nc.vector.memset(rest[:, 0:1], 0.0)
+        w_pairs = late.tile([P, N], BF16, offset=24 * KIB, name="w_pairs")
+        p = [keep.tile([P, N + 4], F32, name="p0"), keep.tile([P, N + 4], F32, name="p1")]
         v_bf = [v0_and_posb[:, 0:N], keep.tile([P, N], BF16, name="v_bf1")[:]]
         v_in = [late.tile([P, 4 * P], BF16, align_bytes=64, offset=19 * KIB, name="v_in0"), keep.tile([P, 4 * P], BF16, align_bytes=64, name="v_in1")]
         v_codes = [keep.tile([P, P], U32, align_bytes=64, name=f"v_codes{v}") for v in range(VB)]
         v_scales = [keep.tile([P, P], U8, align_bytes=64, name=f"v_scales{v}") for v in range(VB)]
-        w_in = [late.tile([P, P, 4], BF16, align_bytes=64, offset=(16 + b) * KIB, name=f"w_in{b}") for b in range(QB)]
+        w_in = [late.tile([P, P, 4], BF16, align_bytes=64, offset=16 * KIB, name="w_in0"), keep.tile([P, P, 4], BF16, align_bytes=64, name="w_in1")]
         w_codes = [keep.tile([P, P], U32, align_bytes=64, name=f"w_codes{b}") for b in range(QB)]
         w_scales = [keep.tile([P, P], U8, align_bytes=64, name=f"w_scales{b}") for b in range(QB)]
         y_sb = [keep.tile([P, QB, P], F32, name=f"y_sb{v}") for v in range(VB)]
@@ -181,7 +184,11 @@ def tile_attend_x_alibi_sink_srt_kernel(tc, qT, kT, vT, vs, pos, slope, sink, of
 
         def softmax(b):
             nc.vector.tensor_reduce(neg_max[b][:], s[b][:, 0 : N + 1], mybir.AxisListType.X, ALU.max, negate=True)
-            nc.scalar.activation(p[b][:, 0 : N + 1], s[b][:, 0 : N + 1], ACT.Exp, bias=neg_max[b][:], accum_out=total[:, b : b + 1])
+            if b == 0:
+                nc.scalar.activation(p[b][:, 0 : N + 1], s[b][:, 0 : N + 1], ACT.Exp, bias=neg_max[b][:], accum_out=total[:, 0:1])
+                return
+            for cols, part in ((slice(0, H), total[:, 1:2]), (slice(H, N + 1), rest[:, 1:2])):
+                nc.scalar.activation(p[b][:, cols], s[b][:, cols], ACT.Exp, bias=neg_max[b][:], accum_out=part)
 
         def gather_values(v, lo, hi, on_vector):
             window = v_raw[v][:].indirect(offsets[:, lo // 16 : hi // 16])
@@ -198,13 +205,18 @@ def tile_attend_x_alibi_sink_srt_kernel(tc, qT, kT, vT, vs, pos, slope, sink, of
             copy(v_in[v][:].bitcast(F32).rearrange("m (e u) -> m e u", u=2), ps[:].rearrange("m u e -> m e u"))
 
         def scale_first_weights():
-            nc.vector.tensor_tensor(w_pairs[:], p[0][:, 0:N], vsb[:].rearrange("q m t -> q (m t)"), ALU.mult)
+            nc.vector.tensor_tensor(
+                w_pairs[:].rearrange("q (u m j) -> q m u j", u=2, j=2),
+                p[0][:, 0:N].rearrange("q (m u j) -> q m u j", u=2, j=2),
+                vsb[:].rearrange("q m (u j) -> q m u j", u=2),
+                ALU.mult,
+            )
 
         def turn_first_weights():
             ps = psum.tile([P, 2, P], F32, tag="p1", name="w_ps")
             words = w_pairs[:].bitcast(F32)
             for u in range(2):
-                nc.tensor.transpose(ps[:, u, :], words[:, u::2], ident[:])
+                nc.tensor.transpose(ps[:, u, :], words[:, u * P : (u + 1) * P], ident[:])
             nc.scalar.copy(w_in[0][:].rearrange("m q t -> m (q t)").bitcast(F32).rearrange("m (q u) -> m q u", u=2), ps[:].rearrange("m u q -> m q u"))
 
         def turn_weights(b):
@@ -262,8 +274,9 @@ def tile_attend_x_alibi_sink_srt_kernel(tc, qT, kT, vT, vs, pos, slope, sink, of
         turn_first_weights()
         turn_values(1, nc.scalar.copy)
         quantise_values(0)
+        nc.vector.tensor_tensor(both[:], total[:], rest[:], ALU.add)
         quantise_weights(0)
-        nc.vector.reciprocal(inv[:], total[:])
+        nc.vector.reciprocal(inv[:], both[:])
         quantise_weights(1)
         product(0, 0)
         product(1, 0)

@@ -35,12 +35,12 @@ def tile_attend_x_alibi_sink_srt_kernel(tc, qT, kT, vT, vs, pos, slope, sink, of
 
         offsets = keep.tile([P, N // 16], U16, name="offsets")
         first, second = offsets[:, 0 : H // 16], offsets[:, H // 16 : N // 16]
-        k_raw = [keep.tile([P, T], F32, name=f"k_raw{t}") for t in range(4)]
-        q_raw = late.tile([P, 4, NQ], F32, offset=2 * KIB, name="q_raw")
-        v_raw = [late.tile([P, T], F32, offset=(8 + 8 * b) * KIB, name=f"v_raw{b}") for b in range(VB)]
+        k_raw = [keep.tile([P, T], F32, align_bytes=256, name=f"k_raw{t}") for t in range(4)]
+        q_raw = late.tile([P, 4, NQ], F32, align_bytes=256, offset=2 * KIB, name="q_raw")
+        v_raw = [late.tile([P, T], F32, align_bytes=256, offset=(8 + 8 * b) * KIB, name=f"v_raw{b}") for b in range(VB)]
         rows = keep.tile([P, P], F32, align_bytes=64, tag="rows", name="rows")
-        pos_raw = keep.tile([P, T], F32, name="pos_raw")
-        vs_raw = keep.tile([P, T], F32, name="vs_raw")
+        pos_raw = keep.tile([P, T], F32, align_bytes=256, name="pos_raw")
+        vs_raw = keep.tile([P, T], F32, align_bytes=256, name="vs_raw")
         k_planes = kT.rearrange("(p t) n -> p t n", t=4)
         nc.sync.dma_start(k_raw[0][:], k_planes[:, 0, :])
         nc.sync.dma_start(offsets[:], offs)
@@ -158,7 +158,7 @@ def tile_attend_x_alibi_sink_srt_kernel(tc, qT, kT, vT, vs, pos, slope, sink, of
         w_in = [late.tile([P, P, 4], BF16, align_bytes=64, offset=16 * KIB, name="w_in0"), keep.tile([P, P, 4], BF16, align_bytes=64, name="w_in1")]
         w_codes = [keep.tile([P, P], U32, align_bytes=64, name=f"w_codes{b}") for b in range(QB)]
         w_scales = [keep.tile([P, P], U8, align_bytes=64, name=f"w_scales{b}") for b in range(QB)]
-        y_sb = [keep.tile([P, QB, P], F32, name=f"y_sb{v}") for v in range(VB)]
+        y_sb = [keep.tile([P, QB, P], F32, align_bytes=256, name=f"y_sb{v}") for v in range(VB)]
 
         def add_bias(b):
             for h in range(2):

@@ -18,7 +18,7 @@ QB = NQ // P
 VB = DV // P
 H = N // 2
 PRE = T - H
-R0 = P - 4
+R0 = P // 2 - 2 * QB
 LEAD = 448
 SHARE = 288
 KIB = 1024
@@ -35,23 +35,23 @@ def tile_attend_x_alibi_sink_srt_kernel(tc, qT, kT, vT, vs, pos, slope, sink, of
 
         offsets = keep.tile([P, N // 16], U16, name="offsets")
         first, second = offsets[:, 0 : H // 16], offsets[:, H // 16 : N // 16]
-        k_raw = [keep.tile([P, T], F32, align_bytes=256, name=f"k_raw{t}") for t in range(4)]
-        q_raw = late.tile([P, 4, NQ], F32, align_bytes=256, offset=2 * KIB, name="q_raw")
-        v_raw = [late.tile([P, T], F32, align_bytes=256, offset=(8 + 8 * b) * KIB, name=f"v_raw{b}") for b in range(VB)]
-        rows = keep.tile([P, P], F32, align_bytes=64, tag="rows", name="rows")
+        k_raw = [late.tile([P, T], F32, align_bytes=256, offset=(16 + 8 * t) * KIB, name=f"k_raw{t}") for t in range(4)]
+        q_raw = late.tile([P, 4, NQ], F32, align_bytes=256, offset=12 * KIB, name="q_raw")
+        v_raw = [late.tile([P, T], F32, align_bytes=256, offset=(48 + 8 * b) * KIB, name=f"v_raw{b}") for b in range(VB)]
+        rows = keep.tile([P, P], F32, name="rows")
         pos_raw = keep.tile([P, T], F32, align_bytes=256, name="pos_raw")
         vs_raw = keep.tile([P, T], F32, align_bytes=256, name="vs_raw")
         k_planes = kT.rearrange("(p t) n -> p t n", t=4)
         nc.sync.dma_start(k_raw[0][:], k_planes[:, 0, :])
         nc.sync.dma_start(offsets[:], offs)
-        nc.scalar.dma_start(vs_raw[P - 1 : P, :], vs[0:1, :])
         nc.scalar.dma_start(pos_raw[P - 1 : P, :], pos[0:1, :])
+        nc.scalar.dma_start(vs_raw[P - 1 : P, :], vs[0:1, :])
+        nc.sync.dma_start(rows[R0 : R0 + QB, :], slope.rearrange("o (b p) x -> (o b) (p x)", p=P))
+        nc.sync.dma_start(rows[R0 + QB : R0 + 2 * QB, :], sink.rearrange("o (b p) x -> (o b) (p x)", p=P))
         nc.sync.dma_start(k_raw[1][:], k_planes[:, 1, :])
         nc.sync.dma_start(k_raw[2][:], k_planes[:, 2, :])
         nc.sync.dma_start(k_raw[3][:, 0:PRE], k_planes[:, 3, 0:PRE])
         nc.sync.dma_start(k_raw[3][:, PRE:T], k_planes[:, 3, PRE:T])
-        nc.sync.dma_start(rows[R0 : R0 + 2, :], slope.rearrange("o (b p) x -> (o b) (p x)", p=P))
-        nc.sync.dma_start(rows[R0 + 2 : R0 + 4, :], sink.rearrange("o (b p) x -> (o b) (p x)", p=P))
         nc.sync.dma_start(q_raw[:], qT.rearrange("o (p t) n -> p (o t) n", t=4))
         for b in range(VB):
             nc.sync.dma_start(v_raw[b][:], vT[b * P : (b + 1) * P, :])
@@ -62,72 +62,82 @@ def tile_attend_x_alibi_sink_srt_kernel(tc, qT, kT, vT, vs, pos, slope, sink, of
 
         nc.vector.memset(vs_raw[0 : P - 1, :], 0.0)
         nc.vector.memset(rows[0:R0, :], 0.0)
+        nc.vector.memset(rows[P // 2 : P, :], 0.0)
         ident = keep.tile([P, P], F32, name="ident")
         make_identity(nc, ident[:])
         nc.gpsimd.memset(pos_raw[0 : P - 1, :], 0.0)
 
+        pos_g = keep.tile([P, N], F32, name="pos_g")
+        nc.vector.tensor_copy(pos_g[:], pos_raw[:].indirect(offsets[:]))
         vs_g = keep.tile([P, N], F32, name="vs_g")
         nc.scalar.activation(vs_g[:], vs_raw[:].indirect(offsets[:]), ACT.Copy)
-        pos_g = keep.tile([P, N], F32, name="pos_g")
-        nc.scalar.activation(pos_g[:], pos_raw[:].indirect(offsets[:]), ACT.Copy)
-        vsT_ps = psum.tile([P, 4, P], F32, tag="p2", name="vsT_ps")
+        posT_ps = psum.tile([P, 4, P], F32, tag="p0", name="posT_ps")
+        for j in range(4):
+            nc.tensor.transpose(posT_ps[:, j, :], pos_g[:, j * P : (j + 1) * P], ident[:])
+        posT = keep.tile([P, 4], F32, name="posT")
+        nc.scalar.copy(posT[:], posT_ps[:, :, P - 1])
+
+        k_in = [keep.tile([P, H, 4], BF16, align_bytes=64, name=f"k_in{h}") for h in range(2)]
+        s = [keep.tile([P, N + 4], F32, align_bytes=64, name="s0"), late.tile([P, N + 4], F32, align_bytes=64, offset=2 * KIB, name="s1")]
+        rows_ps = psum.tile([P, P], F32, tag="p0", name="rows_ps")
+        nc.tensor.transpose(rows_ps[:], rows[:], ident[:])
+        slopes = keep.tile([P, QB], F32, name="slopes")
+        nc.scalar.copy(slopes[:], rows_ps[:, R0 : R0 + QB])
+        for b in range(QB):
+            nc.scalar.copy(s[b][:, N : N + 1], rows_ps[:, R0 + QB + b : R0 + QB + b + 1])
+
+        posb_ps = psum.tile([P, N], F32, tag="p1", name="posb_ps")
+        for j in range(4):
+            nc.tensor.transpose(posb_ps[:, j * P : (j + 1) * P], posT[:, j : j + 1].to_broadcast([P, P]), ident[:])
+        v0_and_bias = late.tile([P, LEAD + 2 * N], BF16, offset=32 * KIB, name="v0_and_bias")
+        bias = [keep.tile([P, N], F32, name="bias0")[:], v0_and_bias[:, LEAD : LEAD + 2 * N].bitcast(F32)]
+        nc.scalar.activation(bias[0], posb_ps[:], ACT.Copy, scale=slopes[:, 0:1])
+        nc.scalar.activation(bias[1].rearrange("q (t m) -> q t m", t=4), posb_ps[:].rearrange("q (m t) -> q t m", t=4), ACT.Copy, scale=slopes[:, 1:2])
+        vsT_ps = psum.tile([P, 4, P], F32, tag="p0", name="vsT_ps")
         for t in range(4):
             nc.tensor.transpose(vsT_ps[:, t, :], vs_g[:, t::4], ident[:])
         vsT = keep.tile([P, 4], F32, name="vsT")
         nc.scalar.copy(vsT[:], vsT_ps[:, :, P - 1])
-        vsb_ps = psum.tile([P, 4, P], F32, tag="s00", name="vsb_ps")
+        vsb_ps = psum.tile([P, 4, P], F32, tag="p3", name="vsb_ps")
         for t in range(4):
             nc.tensor.transpose(vsb_ps[:, t, :], vsT[:, t : t + 1].to_broadcast([P, P]), ident[:])
-        vsb = keep.tile([P, P, 4], F32, name="vsb")
-        nc.scalar.copy(vsb[:], vsb_ps[:].rearrange("q t m -> q m t"))
-        posT_ps = psum.tile([P, 4, P], F32, tag="p0", name="posT_ps")
-        for t in range(4):
-            nc.tensor.transpose(posT_ps[:, t, :], pos_g[:, t::4], ident[:])
-        posT = keep.tile([P, 4], F32, align_bytes=64, tag="posT", name="posT")
-        nc.scalar.copy(posT[:], posT_ps[:, :, P - 1])
-        posb_ps = psum.tile([P, 4, P], F32, tag="p1", name="posb_ps")
-        for t in range(4):
-            nc.tensor.transpose(posb_ps[:, t, :], posT[:, t : t + 1].to_broadcast([P, P]), ident[:])
-        v0_and_posb = keep.tile([P, LEAD + 2 * N], BF16, name="v0_and_posb")
-        posb = v0_and_posb[:, LEAD : LEAD + 2 * N].bitcast(F32).rearrange("q (t m) -> q t m", t=4)
-        nc.scalar.copy(posb, posb_ps[:])
-        posn = keep.tile([P, P, 4], F32, name="posn")
-        nc.scalar.copy(posn[:], posb_ps[:].rearrange("q t m -> q m t"))
 
-        k_in = [keep.tile([P, H, 4], BF16, align_bytes=64, tag="posT", name="k_in0"), keep.tile([P, H, 4], BF16, align_bytes=64, name="k_in1")]
+        q_in = [keep.tile([P, P, 4], BF16, align_bytes=64, name="q_in0"), keep.tile([P, P, 4], BF16, align_bytes=64, name="q_in1")]
+        q_codes = [keep.tile([P, P], U32, align_bytes=64, name=f"q_codes{b}") for b in range(QB)]
+        q_scales = [keep.tile([P, P], U8, align_bytes=64, name="q_scales0"), keep.tile([P, P], U8, align_bytes=64, name="q_scales1")]
+        k_codes = keep.tile([P, N], U32, align_bytes=64, name="k_codes")
+        k_scales = keep.tile([P, N], U8, align_bytes=64, name="k_scales")
+
+        def gather_keys(t):
+            window = k_raw[t][:, 0:PRE] if t == 3 else k_raw[t][:]
+            nc.vector.tensor_copy(k_in[0][:, :, t], window.indirect(first))
+            if t < 3:
+                nc.vector.tensor_copy(k_pairs[:, t // 2, :, t % 2], k_raw[t][:].indirect(second))
+            else:
+                nc.scalar.activation(k_pairs[:, t // 2, :, t % 2], k_raw[t][:].indirect(second), ACT.Copy)
+
         k_pairs = keep.tile([P, 2, H, 2], BF16, name="k_pairs")
         for t in range(4):
-            window = k_raw[t][:, 0:PRE] if t == 3 else k_raw[t][:]
-            nc.vector.tensor_copy(k_pairs[:, t // 2, :, t % 2], window.indirect(first))
-            nc.vector.tensor_copy(k_in[1][:, :, t], k_raw[t][:].indirect(second))
-        nc.scalar.copy(
-            k_in[0][:].rearrange("p n t -> p (n t)").bitcast(F32).rearrange("p (n u) -> p n u", u=2),
+            gather_keys(t)
+        nc.vector.tensor_copy(
+            k_in[1][:].rearrange("p n t -> p (n t)").bitcast(F32).rearrange("p (n u) -> p n u", u=2),
             k_pairs[:].rearrange("p u n j -> p (u n j)").bitcast(F32).rearrange("p (u n) -> p n u", u=2),
         )
-
-        q_in = [keep.tile([P, P, 4], BF16, align_bytes=64, name=f"q_in{b}") for b in range(QB)]
-        for b in range(QB):
-            nc.scalar.copy(
-                q_in[b][:].rearrange("p (c i) t -> p c t i", i=4),
-                q_raw[:, :, b * P : (b + 1) * P].rearrange("p t (c i) -> p c t i", i=4),
-            )
-        s = [late.tile([P, N + 4], F32, align_bytes=64, offset=4 * KIB * b, name=f"s{b}") for b in range(QB)]
-        slope_ps = psum.tile([P, P], F32, tag="p3", name="slope_ps")
-        nc.tensor.transpose(slope_ps[:], rows[:], ident[:])
-        sink_ps = psum.tile([P, P], F32, tag="p2", name="sink_ps")
-        nc.tensor.transpose(sink_ps[:], rows[:], ident[:])
-        for b in range(QB):
-            nc.scalar.copy(s[b][:, N : N + 1], sink_ps[:, R0 + QB + b : R0 + QB + b + 1])
-
-        k_codes = keep.tile([P, N], U32, align_bytes=64, name="k_codes")
-        k_scales = keep.tile([P, N], U8, align_bytes=64, tag="rows", name="k_scales")
         for h in range(2):
             ks = slice(h * H, (h + 1) * H)
             nc.vector.quantize_mx(out=k_codes[:, ks].bitcast(FP8X4), scales=k_scales[:, ks], in_=k_in[h][:].rearrange("p n t -> p (n t)"))
-        q_codes = [keep.tile([P, P], U32, align_bytes=64, name=f"q_codes{b}") for b in range(QB)]
-        q_scales = [keep.tile([P, P], U8, align_bytes=64, name=f"q_scales{b}") for b in range(QB)]
+
+        def weave_queries(copy, lo, hi):
+            b = lo // P
+            copy(q_in[b][:, lo - b * P : hi - b * P, :].rearrange("p (c i) t -> p c t i", i=4), q_raw[:, :, lo:hi].rearrange("p t (c i) -> p c t i", i=4))
+
+        weave_queries(nc.scalar.copy, 0, P)
+        weave_queries(nc.scalar.copy, P, NQ)
         for b in range(QB):
             nc.vector.quantize_mx(out=q_codes[b][:].bitcast(FP8X4), scales=q_scales[b][:], in_=q_in[b][:].rearrange("p n t -> p (n t)"))
+
+        vsb = late.tile([P, P, 4], F32, offset=12 * KIB, name="vsb")
+        nc.scalar.copy(vsb[:], vsb_ps[:].rearrange("q t m -> q m t"))
 
         scores = [[psum.tile([P, H], F32, tag=f"s{b}{h}", name=f"scores{b}{h}") for h in range(2)] for b in range(QB)]
         for b in range(QB):
@@ -146,39 +156,31 @@ def tile_attend_x_alibi_sink_srt_kernel(tc, qT, kT, vT, vs, pos, slope, sink, of
         neg_max = [keep.tile([P, 1], F32, name=f"neg_max{b}") for b in range(QB)]
         total = keep.tile([P, QB], F32, name="total")
         inv = keep.tile([P, QB], F32, name="inv")
-        both = late.tile([P, QB], F32, offset=24 * KIB, name="both")
+        both = late.tile([P, QB], F32, offset=64 * KIB, name="both")
         rest = keep.tile([P, QB], F32, name="rest")
         nc.vector.memset(rest[:, 0:1], 0.0)
-        w_pairs = late.tile([P, N], BF16, offset=24 * KIB, name="w_pairs")
+        w_pairs = late.tile([P, N], BF16, offset=64 * KIB, name="w_pairs")
         p = [keep.tile([P, N + 4], F32, name="p0"), keep.tile([P, N + 4], F32, name="p1")]
-        v_bf = [v0_and_posb[:, 0:N], keep.tile([P, N], BF16, name="v_bf1")[:]]
-        v_in = [late.tile([P, 4 * P], BF16, align_bytes=64, offset=19 * KIB, name="v_in0"), keep.tile([P, 4 * P], BF16, align_bytes=64, name="v_in1")]
+        v_bf = [v0_and_bias[:, 0:N], keep.tile([P, N], BF16, name="v_bf1")[:]]
+        v_in = [late.tile([P, 4 * P], BF16, align_bytes=64, offset=59 * KIB, name="v_in0"), keep.tile([P, 4 * P], BF16, align_bytes=64, name="v_in1")]
         v_codes = [keep.tile([P, P], U32, align_bytes=64, name=f"v_codes{v}") for v in range(VB)]
         v_scales = [keep.tile([P, P], U8, align_bytes=64, name=f"v_scales{v}") for v in range(VB)]
-        w_in = [late.tile([P, P, 4], BF16, align_bytes=64, offset=16 * KIB, name="w_in0"), keep.tile([P, P, 4], BF16, align_bytes=64, name="w_in1")]
+        w_in = [late.tile([P, P, 4], BF16, align_bytes=64, offset=56 * KIB, name="w_in0"), keep.tile([P, P, 4], BF16, align_bytes=64, name="w_in1")]
         w_codes = [keep.tile([P, P], U32, align_bytes=64, name=f"w_codes{b}") for b in range(QB)]
         w_scales = [keep.tile([P, P], U8, align_bytes=64, name=f"w_scales{b}") for b in range(QB)]
         y_sb = [keep.tile([P, QB, P], F32, align_bytes=256, name=f"y_sb{v}") for v in range(VB)]
 
         def add_bias(b):
             for h in range(2):
-                ms = slice(h * P // 2, (h + 1) * P // 2)
                 if b == 0:
-                    nc.vector.scalar_tensor_tensor(
-                        s[b][:, h * H : (h + 1) * H],
-                        posn[:, ms, :].rearrange("q m t -> q (m t)"),
-                        slope_ps[:, R0 + b : R0 + b + 1],
-                        scores[b][h][:],
-                        ALU.mult,
-                        ALU.add,
-                    )
+                    cols = slice(h * H, (h + 1) * H)
+                    nc.vector.tensor_tensor(s[b][:, cols], scores[b][h][:], bias[b][:, cols], ALU.add)
                     continue
-                nc.vector.scalar_tensor_tensor(
+                ms = slice(h * P // 2, (h + 1) * P // 2)
+                nc.vector.tensor_tensor(
                     s[b][:, 0:N].rearrange("q (t m) -> q t m", t=4)[:, :, ms],
-                    posb[:, :, ms],
-                    slope_ps[:, R0 + b : R0 + b + 1],
                     scores[b][h][:].rearrange("q (m t) -> q t m", t=4),
-                    ALU.mult,
+                    bias[b].rearrange("q (t m) -> q t m", t=4)[:, :, ms],
                     ALU.add,
                 )
 
@@ -251,7 +253,7 @@ def tile_attend_x_alibi_sink_srt_kernel(tc, qT, kT, vT, vs, pos, slope, sink, of
 
         def finish(v):
             for b in range(QB):
-                if b == 0 or v == 0:
+                if b == 0:
                     nc.scalar.activation(y_sb[v][:, b, :], y[b][v][:], ACT.Copy, scale=inv[:, b : b + 1])
                 else:
                     nc.vector.tensor_scalar(y_sb[v][:, b, :], y[b][v][:], inv[:, b : b + 1], None, ALU.mult)

from contextlib import ExitStack

import concourse.mybir as mybir
from concourse.masks import make_identity

F32 = mybir.dt.float32
BF16 = mybir.dt.bfloat16
U32 = mybir.dt.uint32
U16 = mybir.dt.uint16
U8 = mybir.dt.uint8
FP8X4 = mybir.dt.float8_e4m3fn_x4
ACT = mybir.ActivationFunctionType
ALU = mybir.AluOpType

P = 128
D, NQ, N, T, DV = 512, 256, 512, 2048, 256
QB = NQ // P
VB = DV // P
H = N // 2
PRE = T - H
R0 = P // 2 - 2 * QB
LEAD = 448
SHARE = 288
KIB = 1024
FLOPS = 2 * NQ * N * (D + DV)
BYTES = 4 * (D * NQ + D * T + DV * T + 2 * T + 2 * NQ + NQ * DV) + 2 * P * (N // 16)


def tile_attend_x_alibi_sink_srt_kernel(tc, qT, kT, vT, vs, pos, slope, sink, offs, out):
    nc = tc.nc
    with ExitStack() as ctx:
        keep = ctx.enter_context(tc.tile_pool(name="keep", bufs=1))
        late = ctx.enter_context(tc.tile_pool(name="late", bufs=1))
        psum = ctx.enter_context(tc.psum_pool(name="psum", bufs=1))

        offsets = keep.tile([P, N // 16], U16, name="offsets")
        first, second = offsets[:, 0 : H // 16], offsets[:, H // 16 : N // 16]
        k_raw = [late.tile([P, T], F32, align_bytes=256, offset=(16 + 8 * t) * KIB, name=f"k_raw{t}") for t in range(4)]
        q_raw = late.tile([P, 4, NQ], F32, align_bytes=256, offset=12 * KIB, name="q_raw")
        v_raw = [late.tile([P, T], F32, align_bytes=256, offset=(48 + 8 * b) * KIB, name=f"v_raw{b}") for b in range(VB)]
        rows = keep.tile([P, P], F32, name="rows")
        pos_raw = keep.tile([P, T], F32, align_bytes=256, name="pos_raw")
        vs_raw = keep.tile([P, T], F32, align_bytes=256, name="vs_raw")
        k_planes = kT.rearrange("(p t) n -> p t n", t=4)
        nc.sync.dma_start(k_raw[0][:], k_planes[:, 0, :])
        nc.sync.dma_start(offsets[:], offs)
        nc.scalar.dma_start(pos_raw[P - 1 : P, :], pos[0:1, :])
        nc.scalar.dma_start(vs_raw[P - 1 : P, :], vs[0:1, :])
        nc.sync.dma_start(rows[R0 : R0 + QB, :], slope.rearrange("o (b p) x -> (o b) (p x)", p=P))
        nc.sync.dma_start(rows[R0 + QB : R0 + 2 * QB, :], sink.rearrange("o (b p) x -> (o b) (p x)", p=P))
        nc.sync.dma_start(k_raw[1][:], k_planes[:, 1, :])
        nc.sync.dma_start(k_raw[2][:], k_planes[:, 2, :])
        nc.sync.dma_start(k_raw[3][:, 0:PRE], k_planes[:, 3, 0:PRE])
        nc.sync.dma_start(k_raw[3][:, PRE:T], k_planes[:, 3, PRE:T])
        nc.sync.dma_start(q_raw[:], qT.rearrange("o (p t) n -> p (o t) n", t=4))
        for b in range(VB):
            nc.sync.dma_start(v_raw[b][:], vT[b * P : (b + 1) * P, :])

        warm = keep.tile([P, 1], F32, name="warm")
        nc.vector.memset(warm[:], 0.0)
        nc.scalar.activation(warm[:], warm[:], ACT.Exp)

        nc.vector.memset(vs_raw[0 : P - 1, :], 0.0)
        nc.vector.memset(rows[0:R0, :], 0.0)
        nc.vector.memset(rows[P // 2 : P, :], 0.0)
        ident = keep.tile([P, P], F32, name="ident")
        make_identity(nc, ident[:])
        nc.gpsimd.memset(pos_raw[0 : P - 1, :], 0.0)

        pos_g = keep.tile([P, N], F32, name="pos_g")
        nc.vector.tensor_copy(pos_g[:], pos_raw[:].indirect(offsets[:]))
        vs_g = keep.tile([P, N], F32, name="vs_g")
        nc.scalar.activation(vs_g[:], vs_raw[:].indirect(offsets[:]), ACT.Copy)
        posT_ps = psum.tile([P, 4, P], F32, tag="p0", name="posT_ps")
        for j in range(4):
            nc.tensor.transpose(posT_ps[:, j, :], pos_g[:, j * P : (j + 1) * P], ident[:])
        posT = keep.tile([P, 4], F32, name="posT")
        nc.scalar.copy(posT[:], posT_ps[:, :, P - 1])

        k_in = [keep.tile([P, H, 4], BF16, align_bytes=64, name=f"k_in{h}") for h in range(2)]
        s = [keep.tile([P, N + 4], F32, align_bytes=64, name="s0"), late.tile([P, N + 4], F32, align_bytes=64, offset=2 * KIB, name="s1")]
        rows_ps = psum.tile([P, P], F32, tag="p0", name="rows_ps")
        nc.tensor.transpose(rows_ps[:], rows[:], ident[:])
        slopes = keep.tile([P, QB], F32, name="slopes")
        nc.scalar.copy(slopes[:], rows_ps[:, R0 : R0 + QB])
        for b in range(QB):
            nc.scalar.copy(s[b][:, N : N + 1], rows_ps[:, R0 + QB + b : R0 + QB + b + 1])

        posb_ps = psum.tile([P, N], F32, tag="p1", name="posb_ps")
        for j in range(4):
            nc.tensor.transpose(posb_ps[:, j * P : (j + 1) * P], posT[:, j : j + 1].to_broadcast([P, P]), ident[:])
        v0_and_bias = late.tile([P, LEAD + 2 * N], BF16, offset=32 * KIB, name="v0_and_bias")
        bias = [keep.tile([P, N], F32, name="bias0")[:], v0_and_bias[:, LEAD : LEAD + 2 * N].bitcast(F32)]
        nc.scalar.activation(bias[0], posb_ps[:], ACT.Copy, scale=slopes[:, 0:1])
        nc.scalar.activation(bias[1].rearrange("q (t m) -> q t m", t=4), posb_ps[:].rearrange("q (m t) -> q t m", t=4), ACT.Copy, scale=slopes[:, 1:2])
        vsT_ps = psum.tile([P, 4, P], F32, tag="p0", name="vsT_ps")
        for t in range(4):
            nc.tensor.transpose(vsT_ps[:, t, :], vs_g[:, t::4], ident[:])
        vsT = keep.tile([P, 4], F32, name="vsT")
        nc.scalar.copy(vsT[:], vsT_ps[:, :, P - 1])
        vsb_ps = psum.tile([P, 4, P], F32, tag="p3", name="vsb_ps")
        for t in range(4):
            nc.tensor.transpose(vsb_ps[:, t, :], vsT[:, t : t + 1].to_broadcast([P, P]), ident[:])

        q_in = [keep.tile([P, P, 4], BF16, align_bytes=64, name="q_in0"), keep.tile([P, P, 4], BF16, align_bytes=64, name="q_in1")]
        q_codes = [keep.tile([P, P], U32, align_bytes=64, name=f"q_codes{b}") for b in range(QB)]
        q_scales = [keep.tile([P, P], U8, align_bytes=64, name="q_scales0"), keep.tile([P, P], U8, align_bytes=64, name="q_scales1")]
        k_codes = keep.tile([P, N], U32, align_bytes=64, name="k_codes")
        k_scales = keep.tile([P, N], U8, align_bytes=64, name="k_scales")

        def gather_keys(t):
            window = k_raw[t][:, 0:PRE] if t == 3 else k_raw[t][:]
            nc.vector.tensor_copy(k_in[0][:, :, t], window.indirect(first))
            if t < 3:
                nc.vector.tensor_copy(k_pairs[:, t // 2, :, t % 2], k_raw[t][:].indirect(second))
            else:
                nc.scalar.activation(k_pairs[:, t // 2, :, t % 2], k_raw[t][:].indirect(second), ACT.Copy)

        k_pairs = keep.tile([P, 2, H, 2], BF16, name="k_pairs")
        for t in range(4):
            gather_keys(t)
        nc.vector.tensor_copy(
            k_in[1][:].rearrange("p n t -> p (n t)").bitcast(F32).rearrange("p (n u) -> p n u", u=2),
            k_pairs[:].rearrange("p u n j -> p (u n j)").bitcast(F32).rearrange("p (u n) -> p n u", u=2),
        )
        for h in range(2):
            ks = slice(h * H, (h + 1) * H)
            nc.vector.quantize_mx(out=k_codes[:, ks].bitcast(FP8X4), scales=k_scales[:, ks], in_=k_in[h][:].rearrange("p n t -> p (n t)"))

        def weave_queries(copy, lo, hi):
            b = lo // P
            copy(q_in[b][:, lo - b * P : hi - b * P, :].rearrange("p (c i) t -> p c t i", i=4), q_raw[:, :, lo:hi].rearrange("p t (c i) -> p c t i", i=4))

        weave_queries(nc.scalar.copy, 0, P)
        weave_queries(nc.scalar.copy, P, NQ)
        for b in range(QB):
            nc.vector.quantize_mx(out=q_codes[b][:].bitcast(FP8X4), scales=q_scales[b][:], in_=q_in[b][:].rearrange("p n t -> p (n t)"))

        vsb = late.tile([P, P, 4], F32, offset=12 * KIB, name="vsb")
        nc.scalar.copy(vsb[:], vsb_ps[:].rearrange("q t m -> q m t"))

        scores = [[psum.tile([P, H], F32, tag=f"s{b}{h}", name=f"scores{b}{h}") for h in range(2)] for b in range(QB)]
        for b in range(QB):
            for h in range(2):
                ks = slice(h * H, (h + 1) * H)
                nc.tensor.matmul_mx(
                    out=scores[b][h][:],
                    lhsT=q_codes[b][:].bitcast(FP8X4),
                    lhsT_scale=q_scales[b][:],
                    rhs=k_codes[:, ks].bitcast(FP8X4),
                    rhs_scale=k_scales[:, ks],
                    start=True,
                    stop=True,
                )

        neg_max = [keep.tile([P, 1], F32, name=f"neg_max{b}") for b in range(QB)]
        total = keep.tile([P, QB], F32, name="total")
        inv = keep.tile([P, QB], F32, name="inv")
        both = late.tile([P, QB], F32, offset=64 * KIB, name="both")
        rest = keep.tile([P, QB], F32, name="rest")
        nc.vector.memset(rest[:, 0:1], 0.0)
        w_pairs = late.tile([P, N], BF16, offset=64 * KIB, name="w_pairs")
        p = [keep.tile([P, N + 4], F32, name="p0"), keep.tile([P, N + 4], F32, name="p1")]
        v_bf = [v0_and_bias[:, 0:N], keep.tile([P, N], BF16, name="v_bf1")[:]]
        v_in = [late.tile([P, 4 * P], BF16, align_bytes=64, offset=59 * KIB, name="v_in0"), keep.tile([P, 4 * P], BF16, align_bytes=64, name="v_in1")]
        v_codes = [keep.tile([P, P], U32, align_bytes=64, name=f"v_codes{v}") for v in range(VB)]
        v_scales = [keep.tile([P, P], U8, align_bytes=64, name=f"v_scales{v}") for v in range(VB)]
        w_in = [late.tile([P, P, 4], BF16, align_bytes=64, offset=56 * KIB, name="w_in0"), keep.tile([P, P, 4], BF16, align_bytes=64, name="w_in1")]
        w_codes = [keep.tile([P, P], U32, align_bytes=64, name=f"w_codes{b}") for b in range(QB)]
        w_scales = [keep.tile([P, P], U8, align_bytes=64, name=f"w_scales{b}") for b in range(QB)]
        y_sb = [keep.tile([P, QB, P], F32, align_bytes=256, name=f"y_sb{v}") for v in range(VB)]

        def add_bias(b):
            for h in range(2):
                if b == 0:
                    cols = slice(h * H, (h + 1) * H)
                    nc.vector.tensor_tensor(s[b][:, cols], scores[b][h][:], bias[b][:, cols], ALU.add)
                    continue
                ms = slice(h * P // 2, (h + 1) * P // 2)
                nc.vector.tensor_tensor(
                    s[b][:, 0:N].rearrange("q (t m) -> q t m", t=4)[:, :, ms],
                    scores[b][h][:].rearrange("q (m t) -> q t m", t=4),
                    bias[b].rearrange("q (t m) -> q t m", t=4)[:, :, ms],
                    ALU.add,
                )

        def softmax(b):
            nc.vector.tensor_reduce(neg_max[b][:], s[b][:, 0 : N + 1], mybir.AxisListType.X, ALU.max, negate=True)
            if b == 0:
                nc.scalar.activation(p[b][:, 0 : N + 1], s[b][:, 0 : N + 1], ACT.Exp, bias=neg_max[b][:], accum_out=total[:, 0:1])
                return
            for cols, part in ((slice(0, H), total[:, 1:2]), (slice(H, N + 1), rest[:, 1:2])):
                nc.scalar.activation(p[b][:, cols], s[b][:, cols], ACT.Exp, bias=neg_max[b][:], accum_out=part)

        def gather_values(v, lo, hi, on_vector):
            window = v_raw[v][:].indirect(offsets[:, lo // 16 : hi // 16])
            if on_vector:
                nc.vector.tensor_copy(v_bf[v][:, lo:hi], window)
            else:
                nc.scalar.activation(v_bf[v][:, lo:hi], window, ACT.Copy)

        def turn_values(v, copy):
            ps = psum.tile([P, 2, P], F32, tag=f"p{3 * v}", name=f"v_ps{v}")
            words = v_bf[v].bitcast(F32)
            for u in range(2):
                nc.tensor.transpose(ps[:, u, :], words[:, u::2], ident[:])
            copy(v_in[v][:].bitcast(F32).rearrange("m (e u) -> m e u", u=2), ps[:].rearrange("m u e -> m e u"))

        def scale_first_weights():
            nc.vector.tensor_tensor(
                w_pairs[:].rearrange("q (u m j) -> q m u j", u=2, j=2),
                p[0][:, 0:N].rearrange("q (m u j) -> q m u j", u=2, j=2),
                vsb[:].rearrange("q m (u j) -> q m u j", u=2),
                ALU.mult,
            )

        def turn_first_weights():
            ps = psum.tile([P, 2, P], F32, tag="p1", name="w_ps")
            words = w_pairs[:].bitcast(F32)
            for u in range(2):
                nc.tensor.transpose(ps[:, u, :], words[:, u * P : (u + 1) * P], ident[:])
            nc.scalar.copy(w_in[0][:].rearrange("m q t -> m (q t)").bitcast(F32).rearrange("m (q u) -> m q u", u=2), ps[:].rearrange("m u q -> m q u"))

        def turn_weights(b):
            ps = psum.tile([P, 4, P], F32, tag=f"p{1 + b}", name=f"p_ps{b}")
            for t in range(4):
                nc.tensor.transpose(ps[:, t, :], p[b][:, t * P : (t + 1) * P], ident[:])
            nc.vector.tensor_tensor(
                w_in[b][:],
                ps[:].rearrange("m t q -> m q t"),
                vsT[:].unsqueeze(1).to_broadcast([P, P, 4]),
                ALU.mult,
            )

        def quantise_weights(b):
            nc.vector.quantize_mx(out=w_codes[b][:].bitcast(FP8X4), scales=w_scales[b][:], in_=w_in[b][:].rearrange("m q t -> m (q t)"))

        def quantise_values(v):
            nc.vector.quantize_mx(out=v_codes[v][:].bitcast(FP8X4), scales=v_scales[v][:], in_=v_in[v][:])

        y = [[psum.tile([P, P], F32, tag=f"s{b}{v}", name=f"y{b}{v}") for v in range(VB)] for b in range(QB)]

        def product(b, v):
            nc.tensor.matmul_mx(
                out=y[b][v][:],
                lhsT=w_codes[b][:].bitcast(FP8X4),
                lhsT_scale=w_scales[b][:],
                rhs=v_codes[v][:].bitcast(FP8X4),
                rhs_scale=v_scales[v][:],
                start=True,
                stop=True,
            )

        def finish(v):
            for b in range(QB):
                if b == 0:
                    nc.scalar.activation(y_sb[v][:, b, :], y[b][v][:], ACT.Copy, scale=inv[:, b : b + 1])
                else:
                    nc.vector.tensor_scalar(y_sb[v][:, b, :], y[b][v][:], inv[:, b : b + 1], None, ALU.mult)
                if v == VB - 1:
                    nc.sync.dma_start(out[0, b * P : (b + 1) * P, v * P : (v + 1) * P], y_sb[v][:, b, :])
            if v < VB - 1:
                nc.sync.dma_start(out.rearrange("o (b q) e -> q (o b) e", q=P)[:, :, v * P : (v + 1) * P], y_sb[v][:])

        gather_values(0, 0, LEAD, False)
        add_bias(0)
        add_bias(1)
        softmax(0)
        softmax(1)
        gather_values(0, LEAD, N, True)
        scale_first_weights()
        gather_values(1, 0, SHARE, True)
        gather_values(1, SHARE, N, False)
        turn_values(0, nc.scalar.copy)
        turn_weights(1)
        turn_first_weights()
        turn_values(1, nc.scalar.copy)
        quantise_values(0)
        nc.vector.tensor_tensor(both[:], total[:], rest[:], ALU.add)
        quantise_weights(0)
        nc.vector.reciprocal(inv[:], both[:])
        quantise_weights(1)
        product(0, 0)
        product(1, 0)
        quantise_values(1)
        product(0, 1)
        product(1, 1)
        finish(0)
        finish(1)
